import numpy as np
import ml_dtypes


def mxq(x, axis, fmt="e4m3"):
    dtype, down = {"e4m3": (ml_dtypes.float8_e4m3fn, 7), "e5m2": (ml_dtypes.float8_e5m2, 14)}[fmt]
    v = np.moveaxis(np.asarray(x, np.float32).astype(ml_dtypes.bfloat16).astype(np.float64), axis, -1)
    blocks = v.reshape(v.shape[:-1] + (-1, 32))
    amax = np.abs(blocks).max(-1, keepdims=True)
    byte = np.maximum(np.where(amax > 0, np.frexp(amax)[1] - 1 + 127, 0) - down, 1)
    scale = np.exp2(byte - 127.0)
    codes = (blocks / scale).astype(np.float32).astype(dtype).astype(np.float64)
    return np.moveaxis((codes * scale).reshape(v.shape), -1, axis)


WIDE = False


def mx_kscale(k):
    if not WIDE:
        return np.ones(k)
    levels = np.array([10, -10, 5, -5, 0])
    if k % 512:
        return np.exp2(np.random.permutation(np.resize(levels, k // 32))).repeat(32)
    a = np.empty((k // 512, 16))
    for p in range(k // 512):
        a[p, :8] = np.random.permutation(np.resize(levels, 8))
        for g in range(8):
            far = levels[np.abs(levels - a[p, g]) >= 10]
            a[p, g + 8] = far[np.random.randint(len(far))]
    return np.exp2(a.ravel()).repeat(32)


def f64(x):
    return np.asarray(x).astype(np.float64)


def striped(idx):
    return np.tile(idx.reshape(-1, 16).T, (8, 1)).astype(np.uint16)


def unstriped(offs):
    return offs[:16].T.reshape(-1).astype(np.int64)


E2M1 = np.array([0.0, 0.5, 1.0, 1.5, 2.0, 3.0, 4.0, 6.0, -0.0, -0.5, -1.0, -1.5, -2.0, -3.0, -4.0, -6.0])


def pack_weight(w, fmt):
    k, n = w.shape
    w = f64(np.asarray(w, np.float32).astype(ml_dtypes.bfloat16)).reshape(k // 32, 32, n)
    amax = np.abs(w).max(1)
    if fmt == "e4m3":
        byte = np.frexp(amax)[1] - 1 + 127 - 7
    else:
        mant, ex = np.frexp(amax / 6.0)
        byte = np.where(mant > 0.5, ex, ex - 1) + 127
    byte = np.clip(np.where(amax > 0, byte, 1), 1, 254)
    scaled = (w * np.exp2(127.0 - byte)[:, None, :]).reshape(k, n).astype(np.float32)
    by_word = np.ascontiguousarray(scaled.reshape(k // 512, 128, 4, n).transpose(0, 1, 3, 2))
    if fmt == "e4m3":
        words = by_word.astype(ml_dtypes.float8_e4m3fn).view(np.uint8)
    else:
        c = by_word.astype(ml_dtypes.float4_e2m1fn).view(np.uint8) & 0xF
        words = (c[..., 0::2] | (c[..., 1::2] << 4)).reshape(k // 512, 128, 2 * n)
    return np.ascontiguousarray(words), np.ascontiguousarray(byte.astype(np.uint8).reshape(k // 512, 16, n))


def unpack_weight(words, scales, fmt):
    g, _, n = scales.shape
    words = np.ascontiguousarray(words).reshape(g, 128, n, -1)
    if fmt == "e4m3":
        vals = words.view(ml_dtypes.float8_e4m3fn).astype(np.float64)
    else:
        nib = np.empty((g, 128, n, 4), np.uint8)
        nib[..., 0::2] = words & 0xF
        nib[..., 1::2] = words >> 4
        vals = E2M1[nib]
    vals = vals * np.repeat(np.exp2(scales.astype(np.float64) - 127.0), 8, axis=1)[..., None]
    return vals.transpose(0, 1, 3, 2).reshape(g * 512, n)


def gelu(v):
    return 0.5 * v * (1.0 + np.tanh(np.sqrt(2.0 / np.pi) * (v + 0.044715 * v**3)))


def striped8(idx):
    return np.concatenate([v.reshape(-1, 16).T for v in idx]).astype(np.uint16)


def unstriped8(offs):
    return np.stack([offs[16 * g:16 * g + 16].T.reshape(-1) for g in range(8)]).astype(np.int64)


def heads(h, wgt, idx8):
    r = np.arange(h.shape[0])
    return wgt[r // 4 % 128] * h[r[:, None], idx8[r % 512 // 64]]


def bf(x):
    return np.asarray(x, np.float32).astype(ml_dtypes.bfloat16)


def planes(Y):
    n, m = Y.shape
    b = f64(bf(Y)).reshape(n // 32, 32, m)
    amax = np.abs(b).max(1)
    byte = np.clip(np.where(amax > 0, np.frexp(amax)[1] - 1 + 127 - 7, 1), 1, 254)
    codes = (b * np.exp2(127.0 - byte)[:, None, :]).reshape(n, m).astype(np.float32).astype(ml_dtypes.float8_e4m3fn).view(np.uint8)
    words = codes.reshape(n // 512, 128, 4, m).transpose(0, 1, 3, 2)
    return np.ascontiguousarray(words), np.ascontiguousarray(byte.astype(np.uint8).reshape(n // 512, 16, m))


K, K2, H, N, T, S, P = 1024, 512, 1024, 512, 2048, 1024, 512

def setup_inputs():
    n = np.random.standard_normal
    s = mx_kscale(K)[:, None]
    s2 = mx_kscale(K2)[:, None]
    u = mx_kscale(H)[:, None]
    tab_words, tab_scales = pack_weight(n((K, T)) * s, "e4m3")
    w4_words, w4_scales = pack_weight(n((K, H)) / np.sqrt(K) / s, "e2m1")
    wm_words, wm_scales = pack_weight(n((H, N)) / np.sqrt(H) / u, "e4m3")
    return {
        "tab_words": tab_words, "tab_scales": tab_scales,
        "offs": striped(np.random.permutation(T)[:S]),
        "w4_words": w4_words, "w4_scales": w4_scales,
        "offs2": striped8(np.stack([np.random.permutation(S)[:P] for _ in range(8)])),
        "wgt": np.repeat(np.random.uniform(0.5, 2.0, (8, P)), 16, axis=0).astype(np.float32),
        "gain": (np.exp(0.3 * n(H)) * u[:, 0]).astype(np.float32),
        "dry": (n((K2, P)) * s2).astype(np.float32),
        "wd": (0.7 * n((K2, H)) / np.sqrt(K2) / s2 * u.T).astype(np.float32),
        "wm_words": wm_words, "wm_scales": wm_scales,
        "bo": (0.4 * n(N)).astype(np.float32),
        "fader": np.exp(0.8 * n(N)).astype(np.float32),
    }

def reference(tab_words, tab_scales, offs, w4_words, w4_scales, offs2, wgt, gain, dry, wd,
              wm_words, wm_scales, bo, fader):
    v = unpack_weight(tab_words, tab_scales, "e4m3")[:, unstriped(offs)]
    w4 = unpack_weight(w4_words, w4_scales, "e2m1")
    wm = unpack_weight(wm_words, wm_scales, "e4m3")
    h = w4.T @ v
    x = heads(h, f64(wgt), unstriped8(offs2))
    wet = np.tanh(x) * f64(gain)[:, None]
    direct = mxq(f64(wd), 0, "e4m3").T @ mxq(f64(dry), 0, "e4m3")
    z = mxq(wet + direct, 0, "e4m3")
    y = ((wm.T @ z) + f64(bo)[:, None]) * f64(fader)[:, None]
    words, scales = planes(y)
    return y, words, scales

@@ -1,0 +1,342 @@
+from contextlib import ExitStack
+
+import concourse.mybir as mybir
+
+K, K2, H, N, T, S, M = 1024, 512, 1024, 512, 2048, 1024, 512
+FLOPS = 2 * (K * H * S + K2 * H * M + H * N * M)
+
+F32 = mybir.dt.float32
+BF16 = mybir.dt.bfloat16
+I32 = mybir.dt.int32
+U32 = mybir.dt.uint32
+U16 = mybir.dt.uint16
+U8 = mybir.dt.uint8
+FP8X4 = mybir.dt.float8_e4m3fn_x4
+FP4X4 = mybir.dt.float4_e2m1fn_x4
+MULT = mybir.AluOpType.mult
+ADD = mybir.AluOpType.add
+ACT = mybir.ActivationFunctionType
+
+P = 128
+PACK = 4
+BANK = 512
+CHUNKS = [(0, 256), (256, 256)]
+WHOLE = (0, M)
+
+
+def tile_list_delay_tap_mixer_kernel(
+    tc, tab_words, tab_scales, offs, w4_words, w4_scales, offs2, wgt, gain, dry, wd,
+    wm_words, wm_scales, bo, fader, out_0, out_1, out_2,
+):
+    nc = tc.nc
+    with ExitStack() as ctx:
+        held = ctx.enter_context(tc.tile_pool(name="held", bufs=1))
+        ring = ctx.enter_context(tc.tile_pool(name="ring", bufs=4))
+        h_psum = ctx.enter_context(tc.psum_pool(name="h_psum", bufs=4))
+        d_psum = ctx.enter_context(tc.psum_pool(name="d_psum", bufs=2))
+        y_psum = ctx.enter_context(tc.psum_pool(name="y_psum", bufs=2))
+
+        def sbuf(shape, dtype, name, tag=None):
+            return held.tile(shape, dtype, name=name, tag=tag or name, align_bytes=64)
+
+        def load_packed_scales(queue, tile, scales, first):
+            for q in range(4):
+                queue.dma_start(
+                    out=tile[32 * q + first : 32 * q + first + 8, :].bitcast(I32),
+                    in_=scales[:, 4 * q : 4 * q + 4, :].bitcast(I32),
+                )
+
+        list1 = held.tile([P, S // 16], U16, name="list1")
+        list2 = held.tile([P, M // 16], U16, name="list2")
+        tab_w = [sbuf([P, T], I32, f"tab_w{a}", tag=f"stage{a}") for a in range(2)]
+        tab_s = sbuf([P, T], U8, "tab_s", tag="stage3")
+        v_w = [[sbuf([P, BANK], U32, f"v_w{a}{jh}") for jh in range(2)] for a in range(2)]
+        v_s = [sbuf([P, S], U8, f"v_s{a}") for a in range(2)]
+
+        w4_raw = sbuf([P, 2, 2 * H], U8, "w4_raw", tag="stage2")
+        w4_w = [sbuf([P, 2, H], U8, f"w4_w{b}") for b in range(2)]
+        w4_sraw = sbuf([P, 2, H], U8, "w4_sraw")
+        w4_s = [sbuf([P, 2, 512], U8, f"w4_s{b}") for b in range(2)]
+        wm_w = sbuf([P, 2, N], I32, "wm_w")
+        wm_sraw = sbuf([P, N], U8, "wm_sraw")
+        wm_s = sbuf([P, N], U8, "wm_s")
+        dry_b = sbuf([P, M, PACK], BF16, "dry_b")
+        dry_w = sbuf([P, M], U32, "dry_w")
+        dry_s = sbuf([P, M], U8, "dry_s")
+        wd_b = [sbuf([P, PACK, P, PACK], BF16, f"wd_b{b}") for b in range(2)]
+        wd_w = [sbuf([P, 512], U32, f"wd_w{b}") for b in range(2)]
+        wd_s = [sbuf([P, 512], U8, f"wd_s{b}") for b in range(2)]
+        wgt_sb = sbuf([P, M], F32, "wgt_sb")
+        gain_sb = sbuf([P, 2, PACK], F32, "gain_sb")
+        bo_sb = sbuf([P, PACK], F32, "bo_sb")
+        fader_sb = sbuf([P, PACK], F32, "fader_sb")
+        bo_faded = sbuf([P, PACK], F32, "bo_faded")
+        h_sb = [sbuf([P, S], F32, f"h_sb{s}") for s in range(8)]
+        y_w = sbuf([P, M], U32, "y_w")
+        y_s = sbuf([P, M], U8, "y_s")
+
+        for tile in (tab_s, w4_sraw, v_s[1], wm_sraw):
+            nc.vector.memset(tile[:].bitcast(I32), 0)
+
+        nc.sync.dma_start(list1[:], offs)
+        load_packed_scales(nc.sync, tab_s, tab_scales, 0)
+        nc.sync.dma_start(out=tab_w[0][:], in_=tab_words[0].rearrange("p t i -> p (t i)").bitcast(I32))
+        for q in range(4):
+            nc.sync.dma_start(
+                out=w4_sraw[32 * q : 32 * q + 4, :, :].bitcast(I32),
+                in_=w4_scales[:, 4 * q : 4 * q + 4, :].rearrange("a r c -> r a c").bitcast(I32),
+            )
+        nc.sync.dma_start(out=w4_raw[:].bitcast(I32), in_=w4_words.rearrange("a p c -> p a c").bitcast(I32))
+        nc.sync.dma_start(out=tab_w[1][:], in_=tab_words[1].rearrange("p t i -> p (t i)").bitcast(I32))
+
+        def gather_words(a, jh):
+            cols = slice(jh * BANK // 16, (jh + 1) * BANK // 16)
+            nc.vector.tensor_copy(v_w[a][jh][:], tab_w[a][:].bitcast(U32).indirect(list1[:, cols]))
+
+        def deal_w4(b):
+            src = w4_raw[:].bitcast(U16)[:, :, 512 * b : 512 * (b + 1)]
+            nc.vector.tensor_copy(
+                out=w4_w[b][:].bitcast(U16).rearrange("p a (t m) -> p a t m", t=PACK),
+                in_=src.rearrange("p a (m t) -> p a t m", t=PACK),
+            )
+
+        def shift_scales(planes):
+            nc.sync.dma_start(out=planes[1][0:112, :].bitcast(I32), in_=planes[0][4:116, :].bitcast(I32))
+
+        wd_raw = {}
+
+        def load_wd(b):
+            wd_raw[b] = sbuf([P, PACK, 512], F32, f"wd_raw{b}", tag=f"stage{b}")
+            nc.sync.dma_start(
+                out=wd_raw[b][:], in_=wd[:, 512 * b : 512 * (b + 1)].rearrange("(p j) c -> p j c", j=PACK)
+            )
+
+        def round_wd(b):
+            nc.scalar.activation(
+                out=wd_b[b][:].rearrange("p t m j -> p m j t"),
+                in_=wd_raw[b][:].rearrange("p j (m t) -> p m j t", t=PACK),
+                func=ACT.Copy,
+            )
+
+        def quantise(words, scales, src):
+            nc.vector.quantize_mx(out=words.bitcast(FP8X4), scales=scales, in_=src)
+
+        nc.vector.tensor_copy(v_s[0][:], tab_s[:].indirect(list1[:]))
+        shift_scales(v_s)
+        dry_raw = sbuf([P, PACK, M], F32, "dry_raw", tag="stage3")
+        nc.sync.dma_start(out=dry_raw[:], in_=dry.rearrange("(p j) m -> p j m", j=PACK))
+        nc.sync.dma_start(list2[:], offs2)
+        nc.sync.dma_start(out=wgt_sb[:], in_=wgt)
+        nc.sync.dma_start(out=gain_sb[:], in_=gain.rearrange("(b p t) -> p b t", b=2, t=PACK))
+        for b in range(2):
+            nc.gpsimd.tensor_copy(
+                out=w4_s[b][:].rearrange("p a (t m) -> p a t m", t=PACK),
+                in_=w4_sraw[:, :, 512 * b : 512 * (b + 1)].rearrange("p a (m t) -> p a t m", t=PACK),
+            )
+        gather_words(0, 0)
+        gather_words(0, 1)
+        load_wd(0)
+        deal_w4(0)
+        gather_words(1, 0)
+        gather_words(1, 1)
+        load_wd(1)
+        nc.vector.tensor_copy(
+            out=dry_b[:].rearrange("p (c i) j -> p c j i", i=4),
+            in_=dry_raw[:].rearrange("p j (c i) -> p c j i", i=4),
+        )
+        quantise(dry_w[:], dry_s[:], dry_b[:].rearrange("p m j -> p (m j)"))
+
+        def make_h(s):
+            b, t = divmod(s, PACK)
+            for jh in range(2):
+                acc = h_psum.tile([P, BANK], F32, name="h_acc")
+                for a in range(2):
+                    nc.tensor.matmul_mx(
+                        out=acc[:],
+                        lhsT=w4_w[b][:, a, 2 * P * t : 2 * P * (t + 1)].bitcast(FP4X4),
+                        lhsT_scale=w4_s[b][:, a, P * t : P * (t + 1)],
+                        rhs=v_w[a][jh][:].bitcast(FP8X4),
+                        rhs_scale=v_s[a][:, BANK * jh : BANK * (jh + 1)],
+                        start=(a == 0),
+                        stop=(a == 1),
+                    )
+                nc.scalar.activation(out=h_sb[s][:, BANK * jh : BANK * (jh + 1)], in_=acc[:], func=ACT.Copy)
+
+        z_rows = [sbuf([P, PACK, M], BF16, "z_rows0")] + [
+            sbuf([P, PACK, w], BF16, f"z_rows1{m0}") for m0, w in CHUNKS
+        ]
+        z_w = [sbuf([P, M], U32, "z_w0")] + [sbuf([P, w], U32, f"z_w1{m0}") for m0, w in CHUNKS]
+        z_s = [sbuf([P, M], U8, "z_s0")] + [sbuf([P, w], U8, f"z_s1{m0}") for m0, w in CHUNKS]
+        spans = [WHOLE] + CHUNKS
+        steps = [(u, t) for u in range(len(spans)) for t in range(PACK)]
+        sats = {}
+        xs = {}
+
+        def pick_taps(u, t):
+            m0, w = spans[u]
+            s = PACK * min(u, 1) + t
+            x = ring.tile([P, w], F32, name="x")
+            nc.vector.tensor_tensor(
+                x[:], h_sb[s][:].indirect(list2[:, m0 // 16 : (m0 + w) // 16]), wgt_sb[:, m0 : m0 + w], MULT
+            )
+            xs[u, t] = x
+
+        def saturate(u, t):
+            sats[u, t] = sbuf([P, spans[u][1]], F32, f"sat{u}{t}")
+            nc.scalar.activation(out=sats[u, t][:], in_=xs[u, t][:], func=ACT.Tanh)
+
+        def add_direct(u, t):
+            m0, w = spans[u]
+            b = min(u, 1)
+            direct = d_psum.tile([P, w], F32, name="direct")
+            nc.tensor.matmul_mx(
+                out=direct[:],
+                lhsT=wd_w[b][:, P * t : P * (t + 1)].bitcast(FP8X4),
+                lhsT_scale=wd_s[b][:, P * t : P * (t + 1)],
+                rhs=dry_w[:, m0 : m0 + w].bitcast(FP8X4),
+                rhs_scale=dry_s[:, m0 : m0 + w],
+                start=True,
+                stop=True,
+            )
+            nc.vector.scalar_tensor_tensor(
+                out=z_rows[u][:, t, :], in0=sats[u, t][:], scalar=gain_sb[:, b, t : t + 1], in1=direct[:],
+                op0=MULT, op1=ADD,
+            )
+
+        z_b = {}
+
+        def weave_z(u, copy):
+            w = spans[u][1]
+            z_b[u] = sbuf([P, w, PACK], BF16, f"z_b{u}")
+            copy(
+                out=z_b[u][:].rearrange("p (c i) t -> p c t i", i=4),
+                in_=z_rows[u][:].rearrange("p t (c i) -> p c t i", i=4),
+            )
+
+        def quantise_z(u):
+            quantise(z_w[u][:], z_s[u][:], z_b[u][:].rearrange("p m t -> p (m t)"))
+
+        def y_pass(acc, c, t, a):
+            m0, w = CHUNKS[c]
+            cols = slice(m0, m0 + w) if a == 0 else slice(0, w)
+            u = 0 if a == 0 else 1 + c
+            nc.tensor.matmul_mx(
+                out=acc,
+                lhsT=wm_w[:, a, P * t : P * (t + 1)].bitcast(FP8X4),
+                lhsT_scale=wm_s[4 * a : P, P * t : P * (t + 1)],
+                rhs=z_w[u][:, cols].bitcast(FP8X4),
+                rhs_scale=z_s[u][:, cols],
+                start=(a == 0),
+                stop=(a == 1),
+            )
+
+        def fade(y, acc, t, on_scalar):
+            if on_scalar:
+                nc.scalar.activation(
+                    out=y[:, t, :], in_=acc, func=ACT.Identity,
+                    scale=fader_sb[:, t : t + 1], bias=bo_faded[:, t : t + 1],
+                )
+            else:
+                nc.vector.tensor_scalar(
+                    out=y[:, t, :], in0=acc, scalar1=bo_sb[:, t : t + 1],
+                    scalar2=fader_sb[:, t : t + 1], op0=ADD, op1=MULT,
+                )
+
+        def finish_y(y, c):
+            m0, w = CHUNKS[c]
+            y_b = sbuf([P, w, PACK], BF16, f"y_b{c}")
+            nc.sync.dma_start(out=out_0[:, m0 : m0 + w].rearrange("(p t) m -> p t m", t=PACK), in_=y[:])
+            nc.vector.tensor_copy(
+                out=y_b[:].rearrange("p (c i) t -> p c t i", i=4),
+                in_=y[:].rearrange("p t (c i) -> p c t i", i=4),
+            )
+            quantise(y_w[:, m0 : m0 + w], y_s[:, m0 : m0 + w], y_b[:].rearrange("p m t -> p (m t)"))
+            nc.sync.dma_start(
+                out=out_1[0].rearrange("p m t -> p (m t)").bitcast(I32)[:, m0 : m0 + w],
+                in_=y_w[:, m0 : m0 + w].bitcast(I32),
+            )
+
+        def quantise_wd(b):
+            round_wd(b)
+            quantise(wd_w[b][:], wd_s[b][:], wd_b[b][:].rearrange("p t m j -> p (t m j)"))
+
+        make_h(0)
+        make_h(1)
+        deal_w4(1)
+        wm_raw = sbuf([P, 2, N], I32, "wm_raw", tag="stage2")
+        nc.sync.dma_start(out=wm_raw[:], in_=wm_words.rearrange("a p c i -> p a (c i)").bitcast(I32))
+        load_packed_scales(nc.sync, wm_sraw, wm_scales, 0)
+        nc.sync.dma_start(out=bo_sb[:], in_=bo.rearrange("(p t) -> p t", t=PACK))
+        nc.sync.dma_start(out=fader_sb[:], in_=fader.rearrange("(p t) -> p t", t=PACK))
+        last = len(CHUNKS) - 1
+        y_tiles = [sbuf([P, PACK, w], F32, f"y{m0}") for m0, w in CHUNKS]
+        make_h(2)
+        pick_taps(0, 0)
+        saturate(0, 0)
+        make_h(3)
+        pick_taps(0, 1)
+        saturate(0, 1)
+        pick_taps(0, 2)
+        pick_taps(0, 3)
+        quantise_wd(0)
+        saturate(0, 2)
+        make_h(4)
+        saturate(0, 3)
+        add_direct(0, 0)
+        add_direct(0, 1)
+        make_h(5)
+        pick_taps(1, 0)
+        add_direct(0, 2)
+        add_direct(0, 3)
+        make_h(6)
+        make_h(7)
+        for t in range(1, PACK):
+            pick_taps(1, t)
+        for t in range(PACK):
+            saturate(1, t)
+        round_wd(1)
+        for t in range(PACK):
+            pick_taps(2, t)
+        for t in range(PACK):
+            saturate(2, t)
+        weave_z(0, nc.scalar.copy)
+        quantise(wd_w[1][:], wd_s[1][:], wd_b[1][:].rearrange("p t m j -> p (t m j)"))
+        nc.vector.tensor_copy(
+            out=wm_w[:].rearrange("p a (t m) -> p a t m", t=PACK),
+            in_=wm_raw[:].rearrange("p a (m t) -> p a t m", t=PACK),
+        )
+        nc.vector.tensor_copy(
+            out=wm_s[:].rearrange("p (t m) -> p t m", t=PACK),
+            in_=wm_sraw[:].rearrange("p (m t) -> p t m", t=PACK),
+        )
+        nc.vector.tensor_tensor(bo_faded[:], bo_sb[:], fader_sb[:], MULT)
+        for t in range(PACK):
+            add_direct(1, t)
+        quantise_z(0)
+        weave_z(1, nc.scalar.copy)
+        last_acc = [h_psum.tile([P, CHUNKS[last][1]], F32, name="h_acc") for t in range(PACK)]
+        for t in range(PACK):
+            add_direct(2, t)
+        quantise_z(1)
+        weave_z(2, nc.vector.tensor_copy)
+        for half in range(2):
+            acc = y_psum.tile([P, 2, CHUNKS[0][1]], F32, name="y_acc")
+            for e in range(2):
+                for a in range(2):
+                    y_pass(acc[:, e, :], 0, 2 * half + e, a)
+            for e in range(2):
+                fade(y_tiles[0], acc[:, e, :], 2 * half + e, True)
+        for t in range(PACK):
+            y_pass(last_acc[t][:], last, t, 0)
+        quantise_z(1 + last)
+        finish_y(y_tiles[0], 0)
+        for t in range(PACK):
+            y_pass(last_acc[t][:], last, t, 1)
+            fade(y_tiles[last], last_acc[t][:], t, t % 2 == 0)
+        finish_y(y_tiles[last], last)
+        for q in range(4):
+            queue = nc.sync if q % 2 == 0 else nc.scalar
+            queue.dma_start(
+                out=out_2[0, 4 * q : 4 * q + 4, :].bitcast(I32),
+                in_=y_s[32 * q : 32 * q + 4, :].bitcast(I32),
+            )

@@ -20,8 +20,7 @@ ACT = mybir.ActivationFunctionType
 P = 128
 PACK = 4
 BANK = 512
-CHUNKS = [(0, 256), (256, 256)]
-WHOLE = (0, M)
+HALF = M // 2
 
 
 def tile_list_delay_tap_mixer_kernel(
@@ -31,10 +30,8 @@ def tile_list_delay_tap_mixer_kernel(
     nc = tc.nc
     with ExitStack() as ctx:
         held = ctx.enter_context(tc.tile_pool(name="held", bufs=1))
-        ring = ctx.enter_context(tc.tile_pool(name="ring", bufs=4))
         h_psum = ctx.enter_context(tc.psum_pool(name="h_psum", bufs=4))
-        d_psum = ctx.enter_context(tc.psum_pool(name="d_psum", bufs=2))
-        y_psum = ctx.enter_context(tc.psum_pool(name="y_psum", bufs=2))
+        d_psum = ctx.enter_context(tc.psum_pool(name="d_psum", bufs=4))
 
         def sbuf(shape, dtype, name, tag=None):
             return held.tile(shape, dtype, name=name, tag=tag or name, align_bytes=64)
@@ -49,16 +46,15 @@ def tile_list_delay_tap_mixer_kernel(
         list1 = held.tile([P, S // 16], U16, name="list1")
         list2 = held.tile([P, M // 16], U16, name="list2")
         tab_w = [sbuf([P, T], I32, f"tab_w{a}", tag=f"stage{a}") for a in range(2)]
-        tab_s = sbuf([P, T], U8, "tab_s", tag="stage3")
-        v_w = [[sbuf([P, BANK], U32, f"v_w{a}{jh}") for jh in range(2)] for a in range(2)]
+        tab_s = sbuf([P, T], U8, "tab_s", tag="stage4")
+        v_w = {}
         v_s = [sbuf([P, S], U8, f"v_s{a}") for a in range(2)]
 
-        w4_raw = sbuf([P, 2, 2 * H], U8, "w4_raw", tag="stage2")
-        w4_w = [sbuf([P, 2, H], U8, f"w4_w{b}") for b in range(2)]
-        w4_sraw = sbuf([P, 2, H], U8, "w4_sraw")
-        w4_s = [sbuf([P, 2, 512], U8, f"w4_s{b}") for b in range(2)]
+        w4_raw = sbuf([P, 2, 2 * H], U8, "w4_raw")
+        w4_w = {}
+        w4_sraw = sbuf([P, 2, H], U8, "w4_sraw", tag="stage2")
+        w4_s = sbuf([P, 2, H], U8, "w4_s")
         wm_w = sbuf([P, 2, N], I32, "wm_w")
-        wm_sraw = sbuf([P, N], U8, "wm_sraw")
         wm_s = sbuf([P, N], U8, "wm_s")
         dry_b = sbuf([P, M, PACK], BF16, "dry_b")
         dry_w = sbuf([P, M], U32, "dry_w")
@@ -68,32 +64,35 @@ def tile_list_delay_tap_mixer_kernel(
         wd_s = [sbuf([P, 512], U8, f"wd_s{b}") for b in range(2)]
         wgt_sb = sbuf([P, M], F32, "wgt_sb")
         gain_sb = sbuf([P, 2, PACK], F32, "gain_sb")
-        bo_sb = sbuf([P, PACK], F32, "bo_sb")
-        fader_sb = sbuf([P, PACK], F32, "fader_sb")
         bo_faded = sbuf([P, PACK], F32, "bo_faded")
         h_sb = [sbuf([P, S], F32, f"h_sb{s}") for s in range(8)]
         y_w = sbuf([P, M], U32, "y_w")
         y_s = sbuf([P, M], U8, "y_s")
 
-        for tile in (tab_s, w4_sraw, v_s[1], wm_sraw):
+        for tile in (tab_s, w4_sraw, v_s[1]):
             nc.vector.memset(tile[:].bitcast(I32), 0)
 
         nc.sync.dma_start(list1[:], offs)
+        nc.sync.dma_start(out=w4_raw[:].bitcast(I32), in_=w4_words.rearrange("a p c -> p a c").bitcast(I32))
         load_packed_scales(nc.sync, tab_s, tab_scales, 0)
-        nc.sync.dma_start(out=tab_w[0][:], in_=tab_words[0].rearrange("p t i -> p (t i)").bitcast(I32))
         for q in range(4):
+            if q == 2:
+                nc.sync.dma_start(out=tab_w[0][:], in_=tab_words[0].rearrange("p t i -> p (t i)").bitcast(I32))
             nc.sync.dma_start(
                 out=w4_sraw[32 * q : 32 * q + 4, :, :].bitcast(I32),
                 in_=w4_scales[:, 4 * q : 4 * q + 4, :].rearrange("a r c -> r a c").bitcast(I32),
             )
-        nc.sync.dma_start(out=w4_raw[:].bitcast(I32), in_=w4_words.rearrange("a p c -> p a c").bitcast(I32))
+        dry_raw = sbuf([P, PACK, M], F32, "dry_raw")
+        nc.sync.dma_start(out=dry_raw[:], in_=dry.rearrange("(p j) m -> p j m", j=PACK))
         nc.sync.dma_start(out=tab_w[1][:], in_=tab_words[1].rearrange("p t i -> p (t i)").bitcast(I32))
 
-        def gather_words(a, jh):
+        def gather_words(a, jh, tag=None):
+            v_w[a, jh] = sbuf([P, BANK], U32, f"v_w{a}{jh}", tag=tag)
             cols = slice(jh * BANK // 16, (jh + 1) * BANK // 16)
-            nc.vector.tensor_copy(v_w[a][jh][:], tab_w[a][:].bitcast(U32).indirect(list1[:, cols]))
+            nc.vector.tensor_copy(v_w[a, jh][:], tab_w[a][:].bitcast(U32).indirect(list1[:, cols]))
 
-        def deal_w4(b):
+        def deal_w4(b, tag=None):
+            w4_w[b] = sbuf([P, 2, H], U8, f"w4_w{b}", tag=tag)
             src = w4_raw[:].bitcast(U16)[:, :, 512 * b : 512 * (b + 1)]
             nc.vector.tensor_copy(
                 out=w4_w[b][:].bitcast(U16).rearrange("p a (t m) -> p a t m", t=PACK),
@@ -121,73 +120,68 @@ def tile_list_delay_tap_mixer_kernel(
         def quantise(words, scales, src):
             nc.vector.quantize_mx(out=words.bitcast(FP8X4), scales=scales, in_=src)
 
+        deal_w4(0)
+        deal_w4(1)
         nc.vector.tensor_copy(v_s[0][:], tab_s[:].indirect(list1[:]))
         shift_scales(v_s)
-        dry_raw = sbuf([P, PACK, M], F32, "dry_raw", tag="stage3")
-        nc.sync.dma_start(out=dry_raw[:], in_=dry.rearrange("(p j) m -> p j m", j=PACK))
         nc.sync.dma_start(list2[:], offs2)
         nc.sync.dma_start(out=wgt_sb[:], in_=wgt)
         nc.sync.dma_start(out=gain_sb[:], in_=gain.rearrange("(b p t) -> p b t", b=2, t=PACK))
-        for b in range(2):
-            nc.gpsimd.tensor_copy(
-                out=w4_s[b][:].rearrange("p a (t m) -> p a t m", t=PACK),
-                in_=w4_sraw[:, :, 512 * b : 512 * (b + 1)].rearrange("p a (m t) -> p a t m", t=PACK),
-            )
         gather_words(0, 0)
-        gather_words(0, 1)
+        nc.vector.tensor_copy(
+            out=w4_s[:].rearrange("p a (b t m) -> p (a b) t m", b=2, t=PACK),
+            in_=w4_sraw[:].rearrange("p a (b m t) -> p (a b) t m", b=2, t=PACK),
+        )
+        gather_words(0, 1, "stage2")
         load_wd(0)
-        deal_w4(0)
         gather_words(1, 0)
         gather_words(1, 1)
-        load_wd(1)
-        nc.vector.tensor_copy(
+        nc.scalar.activation(
             out=dry_b[:].rearrange("p (c i) j -> p c j i", i=4),
             in_=dry_raw[:].rearrange("p j (c i) -> p c j i", i=4),
+            func=ACT.Copy,
         )
+        load_wd(1)
         quantise(dry_w[:], dry_s[:], dry_b[:].rearrange("p m j -> p (m j)"))
 
-        def make_h(s):
+        def h_pass(acc, s, jh, a):
             b, t = divmod(s, PACK)
-            for jh in range(2):
-                acc = h_psum.tile([P, BANK], F32, name="h_acc")
-                for a in range(2):
-                    nc.tensor.matmul_mx(
-                        out=acc[:],
-                        lhsT=w4_w[b][:, a, 2 * P * t : 2 * P * (t + 1)].bitcast(FP4X4),
-                        lhsT_scale=w4_s[b][:, a, P * t : P * (t + 1)],
-                        rhs=v_w[a][jh][:].bitcast(FP8X4),
-                        rhs_scale=v_s[a][:, BANK * jh : BANK * (jh + 1)],
-                        start=(a == 0),
-                        stop=(a == 1),
-                    )
-                nc.scalar.activation(out=h_sb[s][:, BANK * jh : BANK * (jh + 1)], in_=acc[:], func=ACT.Copy)
-
-        z_rows = [sbuf([P, PACK, M], BF16, "z_rows0")] + [
-            sbuf([P, PACK, w], BF16, f"z_rows1{m0}") for m0, w in CHUNKS
-        ]
-        z_w = [sbuf([P, M], U32, "z_w0")] + [sbuf([P, w], U32, f"z_w1{m0}") for m0, w in CHUNKS]
-        z_s = [sbuf([P, M], U8, "z_s0")] + [sbuf([P, w], U8, f"z_s1{m0}") for m0, w in CHUNKS]
-        spans = [WHOLE] + CHUNKS
-        steps = [(u, t) for u in range(len(spans)) for t in range(PACK)]
-        sats = {}
-        xs = {}
-
-        def pick_taps(u, t):
-            m0, w = spans[u]
-            s = PACK * min(u, 1) + t
-            x = ring.tile([P, w], F32, name="x")
-            nc.vector.tensor_tensor(
-                x[:], h_sb[s][:].indirect(list2[:, m0 // 16 : (m0 + w) // 16]), wgt_sb[:, m0 : m0 + w], MULT
+            nc.tensor.matmul_mx(
+                out=acc[:],
+                lhsT=w4_w[b][:, a, 2 * P * t : 2 * P * (t + 1)].bitcast(FP4X4),
+                lhsT_scale=w4_s[:, a, P * s : P * (s + 1)],
+                rhs=v_w[a, jh][:].bitcast(FP8X4),
+                rhs_scale=v_s[a][:, BANK * jh : BANK * (jh + 1)],
+                start=(a == 0),
+                stop=(a == 1),
             )
-            xs[u, t] = x
 
-        def saturate(u, t):
-            sats[u, t] = sbuf([P, spans[u][1]], F32, f"sat{u}{t}")
-            nc.scalar.activation(out=sats[u, t][:], in_=xs[u, t][:], func=ACT.Tanh)
+        def make_h(*slices):
+            banks = [(s, jh, h_psum.tile([P, BANK], F32, name="h_acc")) for jh in range(2) for s in slices]
+            for a in range(2):
+                for s, jh, acc in banks:
+                    h_pass(acc, s, jh, a)
+                    if a == 1:
+                        nc.scalar.activation(out=h_sb[s][:, BANK * jh : BANK * (jh + 1)], in_=acc[:], func=ACT.Copy)
+
+        spans = [(0, 0, M), (1, 0, HALF), (1, HALF, HALF)]
+        taps = [sbuf([P, PACK, M], F32, f"taps{b}") for b in range(2)]
+        sats = [sbuf([P, PACK, M], F32, f"sats{b}") for b in range(2)]
+        z_rows = [sbuf([P, PACK, w], BF16, f"z_rows{u}") for u, (b, m0, w) in enumerate(spans)]
+        z_w = [sbuf([P, w], U32, f"z_w{u}") for u, (b, m0, w) in enumerate(spans)]
+        z_s = [sbuf([P, w], U8, f"z_s{u}") for u, (b, m0, w) in enumerate(spans)]
+        y_rows = [sbuf([P, PACK, HALF], F32, f"y_rows{c}") for c in range(2)]
+
+        def pick_taps(s):
+            b, t = divmod(s, PACK)
+            nc.vector.tensor_tensor(taps[b][:, t, :], h_sb[s][:].indirect(list2[:]), wgt_sb[:], MULT)
+
+        def saturate(s):
+            b, t = divmod(s, PACK)
+            nc.scalar.activation(out=sats[b][:, t, :], in_=taps[b][:, t, :], func=ACT.Tanh)
 
         def add_direct(u, t):
-            m0, w = spans[u]
-            b = min(u, 1)
+            b, m0, w = spans[u]
             direct = d_psum.tile([P, w], F32, name="direct")
             nc.tensor.matmul_mx(
                 out=direct[:],
@@ -199,108 +193,99 @@ def tile_list_delay_tap_mixer_kernel(
                 stop=True,
             )
             nc.vector.scalar_tensor_tensor(
-                out=z_rows[u][:, t, :], in0=sats[u, t][:], scalar=gain_sb[:, b, t : t + 1], in1=direct[:],
-                op0=MULT, op1=ADD,
+                out=z_rows[u][:, t, :], in0=sats[b][:, t, m0 : m0 + w], scalar=gain_sb[:, b, t : t + 1],
+                in1=direct[:], op0=MULT, op1=ADD,
             )
 
-        z_b = {}
-
-        def weave_z(u, copy):
-            w = spans[u][1]
-            z_b[u] = sbuf([P, w, PACK], BF16, f"z_b{u}")
+        def weave(copy, rows, name):
+            woven = sbuf([P, rows.shape[2], PACK], BF16, name)
             copy(
-                out=z_b[u][:].rearrange("p (c i) t -> p c t i", i=4),
-                in_=z_rows[u][:].rearrange("p t (c i) -> p c t i", i=4),
+                out=woven[:].rearrange("p (c i) t -> p c t i", i=4),
+                in_=rows[:].rearrange("p t (c i) -> p c t i", i=4),
             )
+            return woven[:].rearrange("p m t -> p (m t)")
 
-        def quantise_z(u):
-            quantise(z_w[u][:], z_s[u][:], z_b[u][:].rearrange("p m t -> p (m t)"))
-
-        def y_pass(acc, c, t, a):
-            m0, w = CHUNKS[c]
-            cols = slice(m0, m0 + w) if a == 0 else slice(0, w)
-            u = 0 if a == 0 else 1 + c
+        def mix_pass(acc, c, t, a, first):
+            u, cols = (0, slice(HALF * c, HALF * (c + 1))) if a == 0 else (1 + c, slice(0, HALF))
             nc.tensor.matmul_mx(
-                out=acc,
+                out=acc[:],
                 lhsT=wm_w[:, a, P * t : P * (t + 1)].bitcast(FP8X4),
                 lhsT_scale=wm_s[4 * a : P, P * t : P * (t + 1)],
                 rhs=z_w[u][:, cols].bitcast(FP8X4),
                 rhs_scale=z_s[u][:, cols],
-                start=(a == 0),
-                stop=(a == 1),
+                start=first,
+                stop=not first,
             )
 
-        def fade(y, acc, t, on_scalar):
-            if on_scalar:
-                nc.scalar.activation(
-                    out=y[:, t, :], in_=acc, func=ACT.Identity,
-                    scale=fader_sb[:, t : t + 1], bias=bo_faded[:, t : t + 1],
-                )
-            else:
-                nc.vector.tensor_scalar(
-                    out=y[:, t, :], in0=acc, scalar1=bo_sb[:, t : t + 1],
-                    scalar2=fader_sb[:, t : t + 1], op0=ADD, op1=MULT,
-                )
+        def open_y(c, a):
+            banks = [h_psum.tile([P, HALF], F32, name="h_acc") for t in range(PACK)]
+            for t in range(PACK):
+                mix_pass(banks[t], c, t, a, True)
+            return banks
 
-        def finish_y(y, c):
-            m0, w = CHUNKS[c]
-            y_b = sbuf([P, w, PACK], BF16, f"y_b{c}")
-            nc.sync.dma_start(out=out_0[:, m0 : m0 + w].rearrange("(p t) m -> p t m", t=PACK), in_=y[:])
-            nc.vector.tensor_copy(
-                out=y_b[:].rearrange("p (c i) t -> p c t i", i=4),
-                in_=y[:].rearrange("p t (c i) -> p c t i", i=4),
-            )
-            quantise(y_w[:, m0 : m0 + w], y_s[:, m0 : m0 + w], y_b[:].rearrange("p m t -> p (m t)"))
+        def close_y(c, a, banks, on_vector):
+            for t in range(PACK):
+                mix_pass(banks[t], c, t, a, False)
+                if t in on_vector:
+                    nc.vector.tensor_scalar(
+                        out=y_rows[c][:, t, :], in0=banks[t][:], scalar1=bo_sb[:, t : t + 1],
+                        scalar2=fader_sb[:, t : t + 1], op0=ADD, op1=MULT,
+                    )
+                else:
+                    nc.scalar.activation(
+                        out=y_rows[c][:, t, :], in_=banks[t][:], func=ACT.Identity,
+                        scale=fader_sb[:, t : t + 1], bias=bo_faded[:, t : t + 1],
+                    )
+            cols = slice(HALF * c, HALF * (c + 1))
+            nc.sync.dma_start(out=out_0[:, cols].rearrange("(p t) m -> p t m", t=PACK), in_=y_rows[c][:])
+
+        def store_planes(c):
+            cols = slice(HALF * c, HALF * (c + 1))
+            quantise(y_w[:, cols], y_s[:, cols], weave(nc.vector.tensor_copy, y_rows[c], f"y_b{c}"))
             nc.sync.dma_start(
-                out=out_1[0].rearrange("p m t -> p (m t)").bitcast(I32)[:, m0 : m0 + w],
-                in_=y_w[:, m0 : m0 + w].bitcast(I32),
+                out=out_1[0].rearrange("p m t -> p (m t)").bitcast(I32)[:, cols], in_=y_w[:, cols].bitcast(I32)
             )
 
         def quantise_wd(b):
             round_wd(b)
             quantise(wd_w[b][:], wd_s[b][:], wd_b[b][:].rearrange("p t m j -> p (t m j)"))
 
-        make_h(0)
-        make_h(1)
-        deal_w4(1)
-        wm_raw = sbuf([P, 2, N], I32, "wm_raw", tag="stage2")
-        nc.sync.dma_start(out=wm_raw[:], in_=wm_words.rearrange("a p c i -> p a (c i)").bitcast(I32))
-        load_packed_scales(nc.sync, wm_sraw, wm_scales, 0)
-        nc.sync.dma_start(out=bo_sb[:], in_=bo.rearrange("(p t) -> p t", t=PACK))
-        nc.sync.dma_start(out=fader_sb[:], in_=fader.rearrange("(p t) -> p t", t=PACK))
-        last = len(CHUNKS) - 1
-        y_tiles = [sbuf([P, PACK, w], F32, f"y{m0}") for m0, w in CHUNKS]
+        mix = sbuf([P, 2, 2 * PACK], F32, "mix", tag="stage4")
+        bo_sb = mix[:, 0, 0:PACK]
+        fader_sb = mix[:, 1, 0:PACK]
+        nc.sync.dma_start(out=bo_sb, in_=bo.rearrange("(p t) -> p t", t=PACK))
+        nc.sync.dma_start(out=fader_sb, in_=fader.rearrange("(p t) -> p t", t=PACK))
+
+        make_h(0, 1)
         make_h(2)
-        pick_taps(0, 0)
-        saturate(0, 0)
         make_h(3)
-        pick_taps(0, 1)
-        saturate(0, 1)
-        pick_taps(0, 2)
-        pick_taps(0, 3)
+        for s in range(PACK):
+            pick_taps(s)
         quantise_wd(0)
-        saturate(0, 2)
+        wm_raw = sbuf([P, 2, N], I32, "wm_raw", tag="stage0")
+        nc.sync.dma_start(out=wm_raw[:], in_=wm_words.rearrange("a p c i -> p a (c i)").bitcast(I32))
+        saturate(0)
+        saturate(1)
         make_h(4)
-        saturate(0, 3)
+        saturate(2)
+        saturate(3)
         add_direct(0, 0)
         add_direct(0, 1)
         make_h(5)
-        pick_taps(1, 0)
+        pick_taps(4)
         add_direct(0, 2)
         add_direct(0, 3)
         make_h(6)
         make_h(7)
-        for t in range(1, PACK):
-            pick_taps(1, t)
-        for t in range(PACK):
-            saturate(1, t)
-        round_wd(1)
-        for t in range(PACK):
-            pick_taps(2, t)
-        for t in range(PACK):
-            saturate(2, t)
-        weave_z(0, nc.scalar.copy)
-        quantise(wd_w[1][:], wd_s[1][:], wd_b[1][:].rearrange("p t m j -> p (t m j)"))
+        wm_sraw = sbuf([P, N], U8, "wm_sraw", tag="stage2")
+        nc.vector.memset(wm_sraw[:].bitcast(I32), 0)
+        load_packed_scales(nc.sync, wm_sraw, wm_scales, 0)
+        for s in range(5, 8):
+            pick_taps(s)
+        quantise_wd(1)
+        for s in range(PACK, 8):
+            saturate(s)
+        woven0 = weave(nc.scalar.copy, z_rows[0], "z_b0")
         nc.vector.tensor_copy(
             out=wm_w[:].rearrange("p a (t m) -> p a t m", t=PACK),
             in_=wm_raw[:].rearrange("p a (m t) -> p a t m", t=PACK),
@@ -309,31 +294,23 @@ def tile_list_delay_tap_mixer_kernel(
             out=wm_s[:].rearrange("p (t m) -> p t m", t=PACK),
             in_=wm_sraw[:].rearrange("p (m t) -> p t m", t=PACK),
         )
-        nc.vector.tensor_tensor(bo_faded[:], bo_sb[:], fader_sb[:], MULT)
+        nc.vector.tensor_tensor(bo_faded[:], bo_sb, fader_sb, MULT)
         for t in range(PACK):
             add_direct(1, t)
-        quantise_z(0)
-        weave_z(1, nc.scalar.copy)
-        last_acc = [h_psum.tile([P, CHUNKS[last][1]], F32, name="h_acc") for t in range(PACK)]
-        for t in range(PACK):
+        woven1 = weave(nc.vector.tensor_copy, z_rows[1], "z_b1")
+        add_direct(2, 0)
+        quantise(z_w[1][:], z_s[1][:], woven1)
+        quantise(z_w[0][:], z_s[0][:], woven0)
+        banks = open_y(0, 1)
+        for t in range(1, PACK):
             add_direct(2, t)
-        quantise_z(1)
-        weave_z(2, nc.vector.tensor_copy)
-        for half in range(2):
-            acc = y_psum.tile([P, 2, CHUNKS[0][1]], F32, name="y_acc")
-            for e in range(2):
-                for a in range(2):
-                    y_pass(acc[:, e, :], 0, 2 * half + e, a)
-            for e in range(2):
-                fade(y_tiles[0], acc[:, e, :], 2 * half + e, True)
-        for t in range(PACK):
-            y_pass(last_acc[t][:], last, t, 0)
-        quantise_z(1 + last)
-        finish_y(y_tiles[0], 0)
-        for t in range(PACK):
-            y_pass(last_acc[t][:], last, t, 1)
-            fade(y_tiles[last], last_acc[t][:], t, t % 2 == 0)
-        finish_y(y_tiles[last], last)
+        close_y(0, 0, banks, ())
+        woven2 = weave(nc.vector.tensor_copy, z_rows[2], "z_b2")
+        banks = open_y(1, 0)
+        quantise(z_w[2][:], z_s[2][:], woven2)
+        store_planes(0)
+        close_y(1, 1, banks, (3,))
+        store_planes(1)
         for q in range(4):
             queue = nc.sync if q % 2 == 0 else nc.scalar
             queue.dma_start(

@@ -46,14 +46,14 @@ def tile_list_delay_tap_mixer_kernel(
         list1 = held.tile([P, S // 16], U16, name="list1")
         list2 = held.tile([P, M // 16], U16, name="list2")
         tab_w = [sbuf([P, T], I32, f"tab_w{a}", tag=f"stage{a}") for a in range(2)]
-        tab_s = sbuf([P, T], U8, "tab_s", tag="stage4")
+        tab_s = sbuf([P, T], U8, "tab_s", tag="stage3")
         v_w = {}
         v_s = [sbuf([P, S], U8, f"v_s{a}") for a in range(2)]
 
-        w4_raw = sbuf([P, 2, 2 * H], U8, "w4_raw")
+        w4_raw = sbuf([P, 2, 2 * H], U8, "w4_raw", tag="stage4")
         w4_w = {}
         w4_sraw = sbuf([P, 2, H], U8, "w4_sraw", tag="stage2")
-        w4_s = sbuf([P, 2, H], U8, "w4_s")
+        w4_s = [sbuf([P, 2, 512], U8, f"w4_s{b}") for b in range(2)]
         wm_w = sbuf([P, 2, N], I32, "wm_w")
         wm_s = sbuf([P, N], U8, "wm_s")
         dry_b = sbuf([P, M, PACK], BF16, "dry_b")
@@ -82,12 +82,10 @@ def tile_list_delay_tap_mixer_kernel(
                 out=w4_sraw[32 * q : 32 * q + 4, :, :].bitcast(I32),
                 in_=w4_scales[:, 4 * q : 4 * q + 4, :].rearrange("a r c -> r a c").bitcast(I32),
             )
-        dry_raw = sbuf([P, PACK, M], F32, "dry_raw")
-        nc.sync.dma_start(out=dry_raw[:], in_=dry.rearrange("(p j) m -> p j m", j=PACK))
         nc.sync.dma_start(out=tab_w[1][:], in_=tab_words[1].rearrange("p t i -> p (t i)").bitcast(I32))
 
-        def gather_words(a, jh, tag=None):
-            v_w[a, jh] = sbuf([P, BANK], U32, f"v_w{a}{jh}", tag=tag)
+        def gather_words(a, jh):
+            v_w[a, jh] = sbuf([P, BANK], U32, f"v_w{a}{jh}")
             cols = slice(jh * BANK // 16, (jh + 1) * BANK // 16)
             nc.vector.tensor_copy(v_w[a, jh][:], tab_w[a][:].bitcast(U32).indirect(list1[:, cols]))
 
@@ -105,41 +103,42 @@ def tile_list_delay_tap_mixer_kernel(
         wd_raw = {}
 
         def load_wd(b):
-            wd_raw[b] = sbuf([P, PACK, 512], F32, f"wd_raw{b}", tag=f"stage{b}")
+            wd_raw[b] = sbuf([P, PACK, 512], F32, f"wd_raw{b}", tag=("stage0", "stage3")[b])
             nc.sync.dma_start(
                 out=wd_raw[b][:], in_=wd[:, 512 * b : 512 * (b + 1)].rearrange("(p j) c -> p j c", j=PACK)
             )
 
         def round_wd(b):
-            nc.scalar.activation(
+            nc.scalar.copy(
                 out=wd_b[b][:].rearrange("p t m j -> p m j t"),
                 in_=wd_raw[b][:].rearrange("p j (m t) -> p m j t", t=PACK),
-                func=ACT.Copy,
             )
 
         def quantise(words, scales, src):
             nc.vector.quantize_mx(out=words.bitcast(FP8X4), scales=scales, in_=src)
 
         deal_w4(0)
-        deal_w4(1)
         nc.vector.tensor_copy(v_s[0][:], tab_s[:].indirect(list1[:]))
         shift_scales(v_s)
+        dry_raw = sbuf([P, PACK, M], F32, "dry_raw", tag="stage3")
+        nc.sync.dma_start(out=dry_raw[:], in_=dry.rearrange("(p j) m -> p j m", j=PACK))
         nc.sync.dma_start(list2[:], offs2)
         nc.sync.dma_start(out=wgt_sb[:], in_=wgt)
         nc.sync.dma_start(out=gain_sb[:], in_=gain.rearrange("(b p t) -> p b t", b=2, t=PACK))
+        for b in range(2):
+            nc.gpsimd.tensor_copy(
+                out=w4_s[b][:].rearrange("p a (t m) -> p a t m", t=PACK),
+                in_=w4_sraw[:, :, 512 * b : 512 * (b + 1)].rearrange("p a (m t) -> p a t m", t=PACK),
+            )
         gather_words(0, 0)
-        nc.vector.tensor_copy(
-            out=w4_s[:].rearrange("p a (b t m) -> p (a b) t m", b=2, t=PACK),
-            in_=w4_sraw[:].rearrange("p a (b m t) -> p (a b) t m", b=2, t=PACK),
-        )
-        gather_words(0, 1, "stage2")
+        gather_words(0, 1)
         load_wd(0)
         gather_words(1, 0)
         gather_words(1, 1)
-        nc.scalar.activation(
+        deal_w4(1, "stage1")
+        nc.vector.tensor_copy(
             out=dry_b[:].rearrange("p (c i) j -> p c j i", i=4),
             in_=dry_raw[:].rearrange("p j (c i) -> p c j i", i=4),
-            func=ACT.Copy,
         )
         load_wd(1)
         quantise(dry_w[:], dry_s[:], dry_b[:].rearrange("p m j -> p (m j)"))
@@ -149,7 +148,7 @@ def tile_list_delay_tap_mixer_kernel(
             nc.tensor.matmul_mx(
                 out=acc[:],
                 lhsT=w4_w[b][:, a, 2 * P * t : 2 * P * (t + 1)].bitcast(FP4X4),
-                lhsT_scale=w4_s[:, a, P * s : P * (s + 1)],
+                lhsT_scale=w4_s[b][:, a, P * t : P * (t + 1)],
                 rhs=v_w[a, jh][:].bitcast(FP8X4),
                 rhs_scale=v_s[a][:, BANK * jh : BANK * (jh + 1)],
                 start=(a == 0),
@@ -174,7 +173,13 @@ def tile_list_delay_tap_mixer_kernel(
 
         def pick_taps(s):
             b, t = divmod(s, PACK)
-            nc.vector.tensor_tensor(taps[b][:, t, :], h_sb[s][:].indirect(list2[:]), wgt_sb[:], MULT)
+            picked = sbuf([P, M], F32, f"picked{s}")
+            for c in range(2):
+                nc.vector.tensor_copy(
+                    picked[:, HALF * c : HALF * (c + 1)],
+                    h_sb[s][:].indirect(list2[:, HALF * c // 16 : HALF * (c + 1) // 16]),
+                )
+            nc.gpsimd.tensor_tensor(taps[b][:, t, :], picked[:], wgt_sb[:], MULT)
 
         def saturate(s):
             b, t = divmod(s, PACK)
@@ -257,34 +262,21 @@ def tile_list_delay_tap_mixer_kernel(
         nc.sync.dma_start(out=fader_sb, in_=fader.rearrange("(p t) -> p t", t=PACK))
 
         make_h(0, 1)
-        make_h(2)
-        make_h(3)
-        for s in range(PACK):
+        wm_sraw = sbuf([P, N], U8, "wm_sraw", tag="stage2")
+        nc.gpsimd.memset(wm_sraw[:].bitcast(I32), 0)
+        load_packed_scales(nc.sync, wm_sraw, wm_scales, 0)
+        for s in range(2, 8):
+            make_h(s)
+        for s in range(8):
             pick_taps(s)
         quantise_wd(0)
         wm_raw = sbuf([P, 2, N], I32, "wm_raw", tag="stage0")
         nc.sync.dma_start(out=wm_raw[:], in_=wm_words.rearrange("a p c i -> p a (c i)").bitcast(I32))
-        saturate(0)
-        saturate(1)
-        make_h(4)
-        saturate(2)
-        saturate(3)
-        add_direct(0, 0)
-        add_direct(0, 1)
-        make_h(5)
-        pick_taps(4)
-        add_direct(0, 2)
-        add_direct(0, 3)
-        make_h(6)
-        make_h(7)
-        wm_sraw = sbuf([P, N], U8, "wm_sraw", tag="stage2")
-        nc.vector.memset(wm_sraw[:].bitcast(I32), 0)
-        load_packed_scales(nc.sync, wm_sraw, wm_scales, 0)
-        for s in range(5, 8):
-            pick_taps(s)
-        quantise_wd(1)
-        for s in range(PACK, 8):
+        for s in range(8):
             saturate(s)
+        for t in range(PACK):
+            add_direct(0, t)
+        quantise_wd(1)
         woven0 = weave(nc.scalar.copy, z_rows[0], "z_b0")
         nc.vector.tensor_copy(
             out=wm_w[:].rearrange("p a (t m) -> p a t m", t=PACK),

@@ -36,10 +36,10 @@ def tile_list_delay_tap_mixer_kernel(
         def sbuf(shape, dtype, name, tag=None):
             return held.tile(shape, dtype, name=name, tag=tag or name, align_bytes=64)
 
-        def load_packed_scales(queue, tile, scales, first):
+        def load_packed_scales(queue, tile, scales):
             for q in range(4):
                 queue.dma_start(
-                    out=tile[32 * q + first : 32 * q + first + 8, :].bitcast(I32),
+                    out=tile[32 * q : 32 * q + 8, :].bitcast(I32),
                     in_=scales[:, 4 * q : 4 * q + 4, :].bitcast(I32),
                 )
 
@@ -50,7 +50,7 @@ def tile_list_delay_tap_mixer_kernel(
         v_w = {}
         v_s = [sbuf([P, S], U8, f"v_s{a}") for a in range(2)]
 
-        w4_raw = sbuf([P, 2, 2 * H], U8, "w4_raw", tag="stage4")
+        w4_raw = [sbuf([P, 2, H], U8, f"w4_raw{b}") for b in range(2)]
         w4_w = {}
         w4_sraw = sbuf([P, 2, H], U8, "w4_sraw", tag="stage2")
         w4_s = [sbuf([P, 2, 512], U8, f"w4_s{b}") for b in range(2)]
@@ -72,17 +72,27 @@ def tile_list_delay_tap_mixer_kernel(
         for tile in (tab_s, w4_sraw, v_s[1]):
             nc.vector.memset(tile[:].bitcast(I32), 0)
 
+        def load_w4(b):
+            nc.sync.dma_start(
+                out=w4_raw[b][:].bitcast(I32),
+                in_=w4_words[:, :, H * b : H * (b + 1)].rearrange("a p c -> p a c").bitcast(I32),
+            )
+
         nc.sync.dma_start(list1[:], offs)
-        nc.sync.dma_start(out=w4_raw[:].bitcast(I32), in_=w4_words.rearrange("a p c -> p a c").bitcast(I32))
-        load_packed_scales(nc.sync, tab_s, tab_scales, 0)
+        load_w4(0)
+        for r in range(4):
+            nc.sync.dma_start(
+                out=tab_s[r:P:16, :].bitcast(I32),
+                in_=tab_scales.rearrange("a (q r) c -> r q a c", r=4)[r].bitcast(I32),
+            )
+        nc.sync.dma_start(out=tab_w[0][:], in_=tab_words[0].rearrange("p t i -> p (t i)").bitcast(I32))
         for q in range(4):
-            if q == 2:
-                nc.sync.dma_start(out=tab_w[0][:], in_=tab_words[0].rearrange("p t i -> p (t i)").bitcast(I32))
             nc.sync.dma_start(
                 out=w4_sraw[32 * q : 32 * q + 4, :, :].bitcast(I32),
                 in_=w4_scales[:, 4 * q : 4 * q + 4, :].rearrange("a r c -> r a c").bitcast(I32),
             )
         nc.sync.dma_start(out=tab_w[1][:], in_=tab_words[1].rearrange("p t i -> p (t i)").bitcast(I32))
+        load_w4(1)
 
         def gather_words(a, jh):
             v_w[a, jh] = sbuf([P, BANK], U32, f"v_w{a}{jh}")
@@ -91,14 +101,13 @@ def tile_list_delay_tap_mixer_kernel(
 
         def deal_w4(b, tag=None):
             w4_w[b] = sbuf([P, 2, H], U8, f"w4_w{b}", tag=tag)
-            src = w4_raw[:].bitcast(U16)[:, :, 512 * b : 512 * (b + 1)]
             nc.vector.tensor_copy(
                 out=w4_w[b][:].bitcast(U16).rearrange("p a (t m) -> p a t m", t=PACK),
-                in_=src.rearrange("p a (m t) -> p a t m", t=PACK),
+                in_=w4_raw[b][:].bitcast(U16).rearrange("p a (m t) -> p a t m", t=PACK),
             )
 
         def shift_scales(planes):
-            nc.sync.dma_start(out=planes[1][0:112, :].bitcast(I32), in_=planes[0][4:116, :].bitcast(I32))
+            nc.sync.dma_start(out=planes[1][0:112, :].bitcast(I32), in_=planes[0][16:128, :].bitcast(I32))
 
         wd_raw = {}
 
@@ -167,19 +176,13 @@ def tile_list_delay_tap_mixer_kernel(
         taps = [sbuf([P, PACK, M], F32, f"taps{b}") for b in range(2)]
         sats = [sbuf([P, PACK, M], F32, f"sats{b}") for b in range(2)]
         z_rows = [sbuf([P, PACK, w], BF16, f"z_rows{u}") for u, (b, m0, w) in enumerate(spans)]
-        z_w = [sbuf([P, w], U32, f"z_w{u}") for u, (b, m0, w) in enumerate(spans)]
-        z_s = [sbuf([P, w], U8, f"z_s{u}") for u, (b, m0, w) in enumerate(spans)]
+        z_w = [[sbuf([P, HALF], U32, f"z_w{b}{c}") for c in range(2)] for b in range(2)]
+        z_s = [[sbuf([P, HALF], U8, f"z_s{b}{c}") for c in range(2)] for b in range(2)]
         y_rows = [sbuf([P, PACK, HALF], F32, f"y_rows{c}") for c in range(2)]
 
         def pick_taps(s):
             b, t = divmod(s, PACK)
-            picked = sbuf([P, M], F32, f"picked{s}")
-            for c in range(2):
-                nc.vector.tensor_copy(
-                    picked[:, HALF * c : HALF * (c + 1)],
-                    h_sb[s][:].indirect(list2[:, HALF * c // 16 : HALF * (c + 1) // 16]),
-                )
-            nc.gpsimd.tensor_tensor(taps[b][:, t, :], picked[:], wgt_sb[:], MULT)
+            nc.vector.tensor_tensor(taps[b][:, t, :], h_sb[s][:].indirect(list2[:]), wgt_sb[:], MULT)
 
         def saturate(s):
             b, t = divmod(s, PACK)
@@ -206,18 +209,17 @@ def tile_list_delay_tap_mixer_kernel(
             woven = sbuf([P, rows.shape[2], PACK], BF16, name)
             copy(
                 out=woven[:].rearrange("p (c i) t -> p c t i", i=4),
-                in_=rows[:].rearrange("p t (c i) -> p c t i", i=4),
+                in_=rows.rearrange("p t (c i) -> p c t i", i=4),
             )
             return woven[:].rearrange("p m t -> p (m t)")
 
         def mix_pass(acc, c, t, a, first):
-            u, cols = (0, slice(HALF * c, HALF * (c + 1))) if a == 0 else (1 + c, slice(0, HALF))
             nc.tensor.matmul_mx(
                 out=acc[:],
                 lhsT=wm_w[:, a, P * t : P * (t + 1)].bitcast(FP8X4),
                 lhsT_scale=wm_s[4 * a : P, P * t : P * (t + 1)],
-                rhs=z_w[u][:, cols].bitcast(FP8X4),
-                rhs_scale=z_s[u][:, cols],
+                rhs=z_w[a][c][:].bitcast(FP8X4),
+                rhs_scale=z_s[a][c][:],
                 start=first,
                 stop=not first,
             )
@@ -246,7 +248,7 @@ def tile_list_delay_tap_mixer_kernel(
 
         def store_planes(c):
             cols = slice(HALF * c, HALF * (c + 1))
-            quantise(y_w[:, cols], y_s[:, cols], weave(nc.vector.tensor_copy, y_rows[c], f"y_b{c}"))
+            quantise(y_w[:, cols], y_s[:, cols], weave(nc.vector.tensor_copy, y_rows[c][:], f"y_b{c}"))
             nc.sync.dma_start(
                 out=out_1[0].rearrange("p m t -> p (m t)").bitcast(I32)[:, cols], in_=y_w[:, cols].bitcast(I32)
             )
@@ -255,7 +257,7 @@ def tile_list_delay_tap_mixer_kernel(
             round_wd(b)
             quantise(wd_w[b][:], wd_s[b][:], wd_b[b][:].rearrange("p t m j -> p (t m j)"))
 
-        mix = sbuf([P, 2, 2 * PACK], F32, "mix", tag="stage4")
+        mix = sbuf([P, 2, 2 * PACK], F32, "mix", tag="w4_raw1")
         bo_sb = mix[:, 0, 0:PACK]
         fader_sb = mix[:, 1, 0:PACK]
         nc.sync.dma_start(out=bo_sb, in_=bo.rearrange("(p t) -> p t", t=PACK))
@@ -264,7 +266,7 @@ def tile_list_delay_tap_mixer_kernel(
         make_h(0, 1)
         wm_sraw = sbuf([P, N], U8, "wm_sraw", tag="stage2")
         nc.gpsimd.memset(wm_sraw[:].bitcast(I32), 0)
-        load_packed_scales(nc.sync, wm_sraw, wm_scales, 0)
+        load_packed_scales(nc.sync, wm_sraw, wm_scales)
         for s in range(2, 8):
             make_h(s)
         for s in range(8):
@@ -272,15 +274,19 @@ def tile_list_delay_tap_mixer_kernel(
         quantise_wd(0)
         wm_raw = sbuf([P, 2, N], I32, "wm_raw", tag="stage0")
         nc.sync.dma_start(out=wm_raw[:], in_=wm_words.rearrange("a p c i -> p a (c i)").bitcast(I32))
-        for s in range(8):
-            saturate(s)
+        for t in range(PACK):
+            saturate(t)
         for t in range(PACK):
             add_direct(0, t)
         quantise_wd(1)
-        woven0 = weave(nc.scalar.copy, z_rows[0], "z_b0")
+        for t in range(PACK):
+            saturate(PACK + t)
+        woven0 = [
+            weave(nc.scalar.copy, z_rows[0][:, :, HALF * c : HALF * (c + 1)], f"z_b0{c}") for c in range(2)
+        ]
         nc.vector.tensor_copy(
-            out=wm_w[:].rearrange("p a (t m) -> p a t m", t=PACK),
-            in_=wm_raw[:].rearrange("p a (m t) -> p a t m", t=PACK),
+            out=wm_w[:].rearrange("p a (t m) -> p a m t", t=PACK),
+            in_=wm_raw[:].rearrange("p a (m t) -> p a m t", t=PACK),
         )
         nc.vector.tensor_copy(
             out=wm_s[:].rearrange("p (t m) -> p t m", t=PACK),
@@ -289,17 +295,17 @@ def tile_list_delay_tap_mixer_kernel(
         nc.vector.tensor_tensor(bo_faded[:], bo_sb, fader_sb, MULT)
         for t in range(PACK):
             add_direct(1, t)
-        woven1 = weave(nc.vector.tensor_copy, z_rows[1], "z_b1")
-        add_direct(2, 0)
-        quantise(z_w[1][:], z_s[1][:], woven1)
-        quantise(z_w[0][:], z_s[0][:], woven0)
-        banks = open_y(0, 1)
-        for t in range(1, PACK):
+        woven1 = weave(nc.vector.tensor_copy, z_rows[1][:], "z_b10")
+        quantise(z_w[0][0][:], z_s[0][0][:], woven0[0])
+        quantise(z_w[1][0][:], z_s[1][0][:], woven1)
+        banks = open_y(0, 0)
+        close_y(0, 1, banks, ())
+        for t in range(PACK):
             add_direct(2, t)
-        close_y(0, 0, banks, ())
-        woven2 = weave(nc.vector.tensor_copy, z_rows[2], "z_b2")
+        woven2 = weave(nc.vector.tensor_copy, z_rows[2][:], "z_b11")
+        quantise(z_w[0][1][:], z_s[0][1][:], woven0[1])
         banks = open_y(1, 0)
-        quantise(z_w[2][:], z_s[2][:], woven2)
+        quantise(z_w[1][1][:], z_s[1][1][:], woven2)
         store_planes(0)
         close_y(1, 1, banks, (3,))
         store_planes(1)

@@ -19,7 +19,12 @@ ACT = mybir.ActivationFunctionType
 
 P = 128
 PACK = 4
+PASS = P * PACK
 BANK = 512
+GROUP = 16
+QUAD = 32
+QUAD_ROWS = 4
+RUN = 4
 HALF = M // 2
 
 
@@ -33,206 +38,241 @@ def tile_list_delay_tap_mixer_kernel(
         h_psum = ctx.enter_context(tc.psum_pool(name="h_psum", bufs=4))
         d_psum = ctx.enter_context(tc.psum_pool(name="d_psum", bufs=4))
 
-        def sbuf(shape, dtype, name, tag=None):
-            return held.tile(shape, dtype, name=name, tag=tag or name, align_bytes=64)
+        def sbuf(shape, dtype, name, after=None):
+            return held.tile(shape, dtype, name=name, tag=after or name, align_bytes=64)
 
-        def load_packed_scales(queue, tile, scales):
-            for q in range(4):
-                queue.dma_start(
-                    out=tile[32 * q : 32 * q + 8, :].bitcast(I32),
-                    in_=scales[:, 4 * q : 4 * q + 4, :].bitcast(I32),
-                )
-
-        list1 = held.tile([P, S // 16], U16, name="list1")
-        list2 = held.tile([P, M // 16], U16, name="list2")
-        tab_w = [sbuf([P, T], I32, f"tab_w{a}", tag=f"stage{a}") for a in range(2)]
-        tab_s = sbuf([P, T], U8, "tab_s", tag="stage3")
-        v_w = {}
-        v_s = [sbuf([P, S], U8, f"v_s{a}") for a in range(2)]
-
-        w4_raw = [sbuf([P, 2, H], U8, f"w4_raw{b}") for b in range(2)]
-        w4_w = {}
-        w4_sraw = sbuf([P, 2, H], U8, "w4_sraw", tag="stage2")
-        w4_s = [sbuf([P, 2, 512], U8, f"w4_s{b}") for b in range(2)]
-        wm_w = sbuf([P, 2, N], I32, "wm_w")
-        wm_s = sbuf([P, N], U8, "wm_s")
-        dry_b = sbuf([P, M, PACK], BF16, "dry_b")
-        dry_w = sbuf([P, M], U32, "dry_w")
-        dry_s = sbuf([P, M], U8, "dry_s")
-        wd_b = [sbuf([P, PACK, P, PACK], BF16, f"wd_b{b}") for b in range(2)]
-        wd_w = [sbuf([P, 512], U32, f"wd_w{b}") for b in range(2)]
-        wd_s = [sbuf([P, 512], U8, f"wd_s{b}") for b in range(2)]
-        wgt_sb = sbuf([P, M], F32, "wgt_sb")
-        gain_sb = sbuf([P, 2, PACK], F32, "gain_sb")
-        bo_faded = sbuf([P, PACK], F32, "bo_faded")
-        h_sb = [sbuf([P, S], F32, f"h_sb{s}") for s in range(8)]
-        y_w = sbuf([P, M], U32, "y_w")
-        y_s = sbuf([P, M], U8, "y_s")
-
-        for tile in (tab_s, w4_sraw, v_s[1]):
-            nc.vector.memset(tile[:].bitcast(I32), 0)
-
-        def load_w4(b):
-            nc.sync.dma_start(
-                out=w4_raw[b][:].bitcast(I32),
-                in_=w4_words[:, :, H * b : H * (b + 1)].rearrange("a p c -> p a c").bitcast(I32),
-            )
-
-        nc.sync.dma_start(list1[:], offs)
-        load_w4(0)
-        for r in range(4):
-            nc.sync.dma_start(
-                out=tab_s[r:P:16, :].bitcast(I32),
-                in_=tab_scales.rearrange("a (q r) c -> r q a c", r=4)[r].bitcast(I32),
-            )
-        nc.sync.dma_start(out=tab_w[0][:], in_=tab_words[0].rearrange("p t i -> p (t i)").bitcast(I32))
-        for q in range(4):
-            nc.sync.dma_start(
-                out=w4_sraw[32 * q : 32 * q + 4, :, :].bitcast(I32),
-                in_=w4_scales[:, 4 * q : 4 * q + 4, :].rearrange("a r c -> r a c").bitcast(I32),
-            )
-        nc.sync.dma_start(out=tab_w[1][:], in_=tab_words[1].rearrange("p t i -> p (t i)").bitcast(I32))
-        load_w4(1)
-
-        def gather_words(a, jh):
-            v_w[a, jh] = sbuf([P, BANK], U32, f"v_w{a}{jh}")
-            cols = slice(jh * BANK // 16, (jh + 1) * BANK // 16)
-            nc.vector.tensor_copy(v_w[a, jh][:], tab_w[a][:].bitcast(U32).indirect(list1[:, cols]))
-
-        def deal_w4(b, tag=None):
-            w4_w[b] = sbuf([P, 2, H], U8, f"w4_w{b}", tag=tag)
-            nc.vector.tensor_copy(
-                out=w4_w[b][:].bitcast(U16).rearrange("p a (t m) -> p a t m", t=PACK),
-                in_=w4_raw[b][:].bitcast(U16).rearrange("p a (m t) -> p a t m", t=PACK),
-            )
-
-        def shift_scales(planes):
-            nc.sync.dma_start(out=planes[1][0:112, :].bitcast(I32), in_=planes[0][16:128, :].bitcast(I32))
-
-        wd_raw = {}
-
-        def load_wd(b):
-            wd_raw[b] = sbuf([P, PACK, 512], F32, f"wd_raw{b}", tag=("stage0", "stage3")[b])
-            nc.sync.dma_start(
-                out=wd_raw[b][:], in_=wd[:, 512 * b : 512 * (b + 1)].rearrange("(p j) c -> p j c", j=PACK)
-            )
-
-        def round_wd(b):
-            nc.scalar.copy(
-                out=wd_b[b][:].rearrange("p t m j -> p m j t"),
-                in_=wd_raw[b][:].rearrange("p j (m t) -> p m j t", t=PACK),
-            )
-
-        def quantise(words, scales, src):
-            nc.vector.quantize_mx(out=words.bitcast(FP8X4), scales=scales, in_=src)
-
-        deal_w4(0)
-        nc.vector.tensor_copy(v_s[0][:], tab_s[:].indirect(list1[:]))
-        shift_scales(v_s)
-        dry_raw = sbuf([P, PACK, M], F32, "dry_raw", tag="stage3")
-        nc.sync.dma_start(out=dry_raw[:], in_=dry.rearrange("(p j) m -> p j m", j=PACK))
-        nc.sync.dma_start(list2[:], offs2)
-        nc.sync.dma_start(out=wgt_sb[:], in_=wgt)
-        nc.sync.dma_start(out=gain_sb[:], in_=gain.rearrange("(b p t) -> p b t", b=2, t=PACK))
-        for b in range(2):
-            nc.gpsimd.tensor_copy(
-                out=w4_s[b][:].rearrange("p a (t m) -> p a t m", t=PACK),
-                in_=w4_sraw[:, :, 512 * b : 512 * (b + 1)].rearrange("p a (m t) -> p a t m", t=PACK),
-            )
-        gather_words(0, 0)
-        gather_words(0, 1)
-        load_wd(0)
-        gather_words(1, 0)
-        gather_words(1, 1)
-        deal_w4(1, "stage1")
-        nc.vector.tensor_copy(
-            out=dry_b[:].rearrange("p (c i) j -> p c j i", i=4),
-            in_=dry_raw[:].rearrange("p j (c i) -> p c j i", i=4),
-        )
-        load_wd(1)
-        quantise(dry_w[:], dry_s[:], dry_b[:].rearrange("p m j -> p (m j)"))
-
-        def h_pass(acc, s, jh, a):
-            b, t = divmod(s, PACK)
-            nc.tensor.matmul_mx(
-                out=acc[:],
-                lhsT=w4_w[b][:, a, 2 * P * t : 2 * P * (t + 1)].bitcast(FP4X4),
-                lhsT_scale=w4_s[b][:, a, P * t : P * (t + 1)],
-                rhs=v_w[a, jh][:].bitcast(FP8X4),
-                rhs_scale=v_s[a][:, BANK * jh : BANK * (jh + 1)],
-                start=(a == 0),
-                stop=(a == 1),
-            )
-
-        def make_h(*slices):
-            banks = [(s, jh, h_psum.tile([P, BANK], F32, name="h_acc")) for jh in range(2) for s in slices]
-            for a in range(2):
-                for s, jh, acc in banks:
-                    h_pass(acc, s, jh, a)
-                    if a == 1:
-                        nc.scalar.activation(out=h_sb[s][:, BANK * jh : BANK * (jh + 1)], in_=acc[:], func=ACT.Copy)
-
-        spans = [(0, 0, M), (1, 0, HALF), (1, HALF, HALF)]
-        taps = [sbuf([P, PACK, M], F32, f"taps{b}") for b in range(2)]
-        sats = [sbuf([P, PACK, M], F32, f"sats{b}") for b in range(2)]
-        z_rows = [sbuf([P, PACK, w], BF16, f"z_rows{u}") for u, (b, m0, w) in enumerate(spans)]
-        z_w = [[sbuf([P, HALF], U32, f"z_w{b}{c}") for c in range(2)] for b in range(2)]
-        z_s = [[sbuf([P, HALF], U8, f"z_s{b}{c}") for c in range(2)] for b in range(2)]
-        y_rows = [sbuf([P, PACK, HALF], F32, f"y_rows{c}") for c in range(2)]
-
-        def pick_taps(s):
-            b, t = divmod(s, PACK)
-            nc.vector.tensor_tensor(taps[b][:, t, :], h_sb[s][:].indirect(list2[:]), wgt_sb[:], MULT)
-
-        def saturate(s):
-            b, t = divmod(s, PACK)
-            nc.scalar.activation(out=sats[b][:, t, :], in_=taps[b][:, t, :], func=ACT.Tanh)
-
-        def add_direct(u, t):
-            b, m0, w = spans[u]
-            direct = d_psum.tile([P, w], F32, name="direct")
-            nc.tensor.matmul_mx(
-                out=direct[:],
-                lhsT=wd_w[b][:, P * t : P * (t + 1)].bitcast(FP8X4),
-                lhsT_scale=wd_s[b][:, P * t : P * (t + 1)],
-                rhs=dry_w[:, m0 : m0 + w].bitcast(FP8X4),
-                rhs_scale=dry_s[:, m0 : m0 + w],
-                start=True,
-                stop=True,
-            )
-            nc.vector.scalar_tensor_tensor(
-                out=z_rows[u][:, t, :], in0=sats[b][:, t, m0 : m0 + w], scalar=gain_sb[:, b, t : t + 1],
-                in1=direct[:], op0=MULT, op1=ADD,
-            )
+        def quantise(words, plane, woven):
+            nc.vector.quantize_mx(out=words.bitcast(FP8X4), scales=plane, in_=woven)
 
         def weave(copy, rows, name):
             woven = sbuf([P, rows.shape[2], PACK], BF16, name)
             copy(
-                out=woven[:].rearrange("p (c i) t -> p c t i", i=4),
-                in_=rows.rearrange("p t (c i) -> p c t i", i=4),
+                out=woven[:].rearrange("p (c i) t -> p c t i", i=RUN),
+                in_=rows.rearrange("p t (c i) -> p c t i", i=RUN),
             )
             return woven[:].rearrange("p m t -> p (m t)")
 
-        def mix_pass(acc, c, t, a, first):
-            nc.tensor.matmul_mx(
-                out=acc[:],
-                lhsT=wm_w[:, a, P * t : P * (t + 1)].bitcast(FP8X4),
-                lhsT_scale=wm_s[4 * a : P, P * t : P * (t + 1)],
-                rhs=z_w[a][c][:].bitcast(FP8X4),
-                rhs_scale=z_s[a][c][:],
-                start=first,
-                stop=not first,
+        list1 = held.tile([P, S // GROUP], U16, name="list1")
+        list2 = held.tile([P, M // GROUP], U16, name="list2")
+        tab_w = [sbuf([P, T], I32, f"tab_w{a}") for a in range(2)]
+        tab_s = sbuf([P, T], U8, "tab_s")
+        v_w = [[sbuf([P, BANK], U32, f"v_w{a}{jh}") for jh in range(2)] for a in range(2)]
+        v_s = [sbuf([P, S], U8, f"v_s{a}") for a in range(2)]
+        w4_raw = [sbuf([P, 2, 2 * PASS], U8, f"w4_raw{b}") for b in range(2)]
+        w4_sraw = sbuf([P, 2, H], U8, "w4_sraw")
+        w4_s = [[sbuf([P, PASS], U8, f"w4_s{b}{a}") for a in range(2)] for b in range(2)]
+
+        for plane in (tab_s, w4_sraw, v_s[1]):
+            nc.vector.memset(plane[:].bitcast(I32), 0)
+
+        def load_w4(b):
+            nc.sync.dma_start(
+                out=w4_raw[b][:].bitcast(I32),
+                in_=w4_words[:, :, 2 * PASS * b : 2 * PASS * (b + 1)].rearrange("a p c -> p a c").bitcast(I32),
             )
 
-        def open_y(c, a):
-            banks = [h_psum.tile([P, HALF], F32, name="h_acc") for t in range(PACK)]
+        def load_table(a):
+            nc.sync.dma_start(out=tab_w[a][:], in_=tab_words[a].rearrange("p t i -> p (t i)").bitcast(I32))
+
+        nc.sync.dma_start(list1[:], offs)
+        load_w4(0)
+        for r in range(QUAD_ROWS):
+            nc.sync.dma_start(
+                out=tab_s[r : P : QUAD // 2, :].bitcast(I32),
+                in_=tab_scales.rearrange("a (q r) c -> r q a c", r=QUAD_ROWS)[r].bitcast(I32),
+            )
+        load_table(0)
+        for q in range(P // QUAD):
+            nc.sync.dma_start(
+                out=w4_sraw[QUAD * q : QUAD * q + QUAD_ROWS, :, :].bitcast(I32),
+                in_=w4_scales[:, QUAD_ROWS * q : QUAD_ROWS * (q + 1), :].rearrange("a r c -> r a c").bitcast(I32),
+            )
+        load_table(1)
+        load_w4(1)
+
+        def deal_w4(b, after=None):
+            words = sbuf([P, 2, 2 * PASS], U8, f"w4_w{b}", after)
+            nc.vector.tensor_copy(
+                out=words[:].bitcast(U16).rearrange("p a (t m) -> p a t m", t=PACK),
+                in_=w4_raw[b][:].bitcast(U16).rearrange("p a (m t) -> p a t m", t=PACK),
+            )
+            return words
+
+        def gather_table(a):
+            for jh in range(2):
+                entries = list1[:, jh * BANK // GROUP : (jh + 1) * BANK // GROUP]
+                nc.vector.tensor_copy(v_w[a][jh][:], tab_w[a][:].bitcast(U32).indirect(entries))
+
+        def load_wd(b, after):
+            rows = sbuf([P, PACK, PASS], F32, f"wd_raw{b}", after)
+            nc.sync.dma_start(
+                out=rows[:], in_=wd[:, PASS * b : PASS * (b + 1)].rearrange("(p j) c -> p j c", j=PACK)
+            )
+            return rows
+
+        w4_w = [deal_w4(0)]
+        nc.vector.tensor_copy(v_s[0][:], tab_s[:].indirect(list1[:]))
+        nc.sync.dma_start(
+            out=v_s[1][0 : P - QUAD // 2, :].bitcast(I32), in_=v_s[0][QUAD // 2 : P, :].bitcast(I32)
+        )
+        dry_raw = sbuf([P, PACK, M], F32, "dry_raw", "tab_s")
+        nc.sync.dma_start(out=dry_raw[:], in_=dry.rearrange("(p j) m -> p j m", j=PACK))
+        nc.sync.dma_start(list2[:], offs2)
+        for b in range(2):
+            for a in range(2):
+                nc.gpsimd.tensor_copy(
+                    out=w4_s[b][a][:].rearrange("p (t m) -> p t m", t=PACK),
+                    in_=w4_sraw[:, a, PASS * b : PASS * (b + 1)].rearrange("p (m t) -> p t m", t=PACK),
+                )
+        wgt_sb = sbuf([P, M], F32, "wgt_sb", "w4_sraw")
+        nc.sync.dma_start(out=wgt_sb[:], in_=wgt)
+        gather_table(0)
+        wd_raw = [load_wd(0, "tab_w0")]
+        gather_table(1)
+        w4_w.append(deal_w4(1, "tab_w1"))
+
+        dry_w = sbuf([P, M], U32, "dry_w")
+        dry_s = sbuf([P, M], U8, "dry_s")
+        dry_woven = weave(nc.vector.tensor_copy, dry_raw[:], "dry_woven")
+        wd_raw.append(load_wd(1, "tab_s"))
+        quantise(dry_w[:], dry_s[:], dry_woven)
+
+        wd_w = [sbuf([P, PASS], U32, f"wd_w{b}") for b in range(2)]
+        wd_s = [sbuf([P, PASS], U8, f"wd_s{b}") for b in range(2)]
+
+        def quantise_wd(b):
+            woven = sbuf([P, PACK, P, PACK], BF16, f"wd_woven{b}")
+            nc.scalar.copy(
+                out=woven[:].rearrange("p t m j -> p m j t"),
+                in_=wd_raw[b][:].rearrange("p j (m t) -> p m j t", t=PACK),
+            )
+            quantise(wd_w[b][:], wd_s[b][:], woven[:].rearrange("p t m j -> p (t m j)"))
+
+        vectors = sbuf([P, 3, 2 * PACK], F32, "vectors", "w4_raw1")
+        gain_sb = vectors[:, 0, :]
+        bo_sb = vectors[:, 1, 0:PACK]
+        fader_sb = vectors[:, 2, 0:PACK]
+        nc.sync.dma_start(
+            out=gain_sb.rearrange("p (b t) -> p b t", t=PACK), in_=gain.rearrange("(b p t) -> p b t", b=2, t=PACK)
+        )
+        nc.sync.dma_start(out=bo_sb, in_=bo.rearrange("(p t) -> p t", t=PACK))
+        nc.sync.dma_start(out=fader_sb, in_=fader.rearrange("(p t) -> p t", t=PACK))
+
+        h_sb = [sbuf([P, S], F32, f"h_sb{s}") for s in range(2 * PACK)]
+
+        def make_h(*slices):
+            banks = [(s, jh, h_psum.tile([P, BANK], F32, name="acc")) for jh in range(2) for s in slices]
+            for a in range(2):
+                for s, jh, acc in banks:
+                    b, t = divmod(s, PACK)
+                    nc.tensor.matmul_mx(
+                        out=acc[:],
+                        lhsT=w4_w[b][:, a, 2 * P * t : 2 * P * (t + 1)].bitcast(FP4X4),
+                        lhsT_scale=w4_s[b][a][:, P * t : P * (t + 1)],
+                        rhs=v_w[a][jh][:].bitcast(FP8X4),
+                        rhs_scale=v_s[a][:, BANK * jh : BANK * (jh + 1)],
+                        start=(a == 0),
+                        stop=(a == 1),
+                    )
+                    if a == 1:
+                        nc.scalar.activation(out=h_sb[s][:, BANK * jh : BANK * (jh + 1)], in_=acc[:], func=ACT.Copy)
+
+        make_h(0, 1)
+        for s in range(2, 2 * PACK):
+            make_h(s)
+
+        taps = [sbuf([P, PACK, M], F32, f"taps{b}") for b in range(2)]
+        wet = [sbuf([P, PACK, M], F32, f"wet{b}") for b in range(2)]
+        for s in range(2 * PACK):
+            b, t = divmod(s, PACK)
+            nc.vector.tensor_tensor(taps[b][:, t, :], h_sb[s][:].indirect(list2[:]), wgt_sb[:], MULT)
+
+        def saturate(b):
             for t in range(PACK):
-                mix_pass(banks[t], c, t, a, True)
+                nc.scalar.activation(out=wet[b][:, t, :], in_=taps[b][:, t, :], func=ACT.Tanh)
+
+        def sum_z(b, m0, width):
+            z_rows = sbuf([P, PACK, width], BF16, f"z_rows{b}_{m0}")
+            cols = slice(m0, m0 + width)
+            for t in range(PACK):
+                direct = d_psum.tile([P, width], F32, name="direct")
+                nc.tensor.matmul_mx(
+                    out=direct[:],
+                    lhsT=wd_w[b][:, P * t : P * (t + 1)].bitcast(FP8X4),
+                    lhsT_scale=wd_s[b][:, P * t : P * (t + 1)],
+                    rhs=dry_w[:, cols].bitcast(FP8X4),
+                    rhs_scale=dry_s[:, cols],
+                    start=True,
+                    stop=True,
+                )
+                s = PACK * b + t
+                nc.vector.scalar_tensor_tensor(
+                    out=z_rows[:, t, :], in0=wet[b][:, t, cols], scalar=gain_sb[:, s : s + 1], in1=direct[:],
+                    op0=MULT, op1=ADD,
+                )
+            return z_rows
+
+        quantise_wd(0)
+        wm_raw = sbuf([P, 2, N], I32, "wm_raw", "tab_w0")
+        nc.sync.dma_start(out=wm_raw[:], in_=wm_words.rearrange("a p c i -> p a (c i)").bitcast(I32))
+        wm_sraw = sbuf([P, N], U8, "wm_sraw", "v_w00")
+        nc.gpsimd.memset(wm_sraw[:].bitcast(I32), 0)
+        for q in range(P // QUAD):
+            nc.sync.dma_start(
+                out=wm_sraw[QUAD * q : QUAD * q + 2 * QUAD_ROWS, :].bitcast(I32),
+                in_=wm_scales[:, QUAD_ROWS * q : QUAD_ROWS * (q + 1), :].bitcast(I32),
+            )
+        saturate(0)
+        z_rows0 = sum_z(0, 0, M)
+        quantise_wd(1)
+        saturate(1)
+        z_woven0 = [
+            weave(nc.scalar.copy, z_rows0[:, :, HALF * c : HALF * (c + 1)], f"z_woven0{c}") for c in range(2)
+        ]
+
+        wm_w = sbuf([P, 2, N], I32, "wm_w")
+        wm_s = sbuf([P, N], U8, "wm_s")
+        bo_faded = sbuf([P, PACK], F32, "bo_faded")
+        nc.vector.tensor_copy(
+            out=wm_w[:].rearrange("p a (t m) -> p a m t", t=PACK),
+            in_=wm_raw[:].rearrange("p a (m t) -> p a m t", t=PACK),
+        )
+        nc.vector.tensor_copy(
+            out=wm_s[:].rearrange("p (t m) -> p t m", t=PACK),
+            in_=wm_sraw[:].rearrange("p (m t) -> p t m", t=PACK),
+        )
+        nc.vector.tensor_tensor(bo_faded[:], bo_sb, fader_sb, MULT)
+
+        z_w = [[sbuf([P, HALF], U32, f"z_w{b}{c}") for c in range(2)] for b in range(2)]
+        z_s = [[sbuf([P, HALF], U8, f"z_s{b}{c}") for c in range(2)] for b in range(2)]
+        y_rows = [sbuf([P, PACK, HALF], F32, f"y_rows{c}") for c in range(2)]
+        y_w = sbuf([P, M], U32, "y_w")
+        y_s = sbuf([P, M], U8, "y_s")
+
+        def mix_pass(acc, c, t, b):
+            nc.tensor.matmul_mx(
+                out=acc[:],
+                lhsT=wm_w[:, b, P * t : P * (t + 1)].bitcast(FP8X4),
+                lhsT_scale=wm_s[QUAD_ROWS * b : P, P * t : P * (t + 1)],
+                rhs=z_w[b][c][:].bitcast(FP8X4),
+                rhs_scale=z_s[b][c][:],
+                start=(b == 0),
+                stop=(b == 1),
+            )
+
+        def open_mix(c):
+            z_rows1 = sum_z(1, HALF * c, HALF)
+            z_woven1 = weave(nc.vector.tensor_copy, z_rows1[:], f"z_woven1{c}")
+            quantise(z_w[0][c][:], z_s[0][c][:], z_woven0[c])
+            banks = [h_psum.tile([P, HALF], F32, name="acc") for t in range(PACK)]
+            for t in range(PACK):
+                mix_pass(banks[t], c, t, 0)
+            quantise(z_w[1][c][:], z_s[1][c][:], z_woven1)
             return banks
 
-        def close_y(c, a, banks, on_vector):
+        def close_mix(c, banks, on_vector):
             for t in range(PACK):
-                mix_pass(banks[t], c, t, a, False)
+                mix_pass(banks[t], c, t, 1)
                 if t in on_vector:
                     nc.vector.tensor_scalar(
                         out=y_rows[c][:, t, :], in0=banks[t][:], scalar1=bo_sb[:, t : t + 1],
@@ -246,72 +286,21 @@ def tile_list_delay_tap_mixer_kernel(
             cols = slice(HALF * c, HALF * (c + 1))
             nc.sync.dma_start(out=out_0[:, cols].rearrange("(p t) m -> p t m", t=PACK), in_=y_rows[c][:])
 
-        def store_planes(c):
+        def store_codes(c):
             cols = slice(HALF * c, HALF * (c + 1))
-            quantise(y_w[:, cols], y_s[:, cols], weave(nc.vector.tensor_copy, y_rows[c][:], f"y_b{c}"))
+            quantise(y_w[:, cols], y_s[:, cols], weave(nc.vector.tensor_copy, y_rows[c][:], f"y_woven{c}"))
             nc.sync.dma_start(
                 out=out_1[0].rearrange("p m t -> p (m t)").bitcast(I32)[:, cols], in_=y_w[:, cols].bitcast(I32)
             )
 
-        def quantise_wd(b):
-            round_wd(b)
-            quantise(wd_w[b][:], wd_s[b][:], wd_b[b][:].rearrange("p t m j -> p (t m j)"))
-
-        mix = sbuf([P, 2, 2 * PACK], F32, "mix", tag="w4_raw1")
-        bo_sb = mix[:, 0, 0:PACK]
-        fader_sb = mix[:, 1, 0:PACK]
-        nc.sync.dma_start(out=bo_sb, in_=bo.rearrange("(p t) -> p t", t=PACK))
-        nc.sync.dma_start(out=fader_sb, in_=fader.rearrange("(p t) -> p t", t=PACK))
-
-        make_h(0, 1)
-        wm_sraw = sbuf([P, N], U8, "wm_sraw", tag="stage2")
-        nc.gpsimd.memset(wm_sraw[:].bitcast(I32), 0)
-        load_packed_scales(nc.sync, wm_sraw, wm_scales)
-        for s in range(2, 8):
-            make_h(s)
-        for s in range(8):
-            pick_taps(s)
-        quantise_wd(0)
-        wm_raw = sbuf([P, 2, N], I32, "wm_raw", tag="stage0")
-        nc.sync.dma_start(out=wm_raw[:], in_=wm_words.rearrange("a p c i -> p a (c i)").bitcast(I32))
-        for t in range(PACK):
-            saturate(t)
-        for t in range(PACK):
-            add_direct(0, t)
-        quantise_wd(1)
-        for t in range(PACK):
-            saturate(PACK + t)
-        woven0 = [
-            weave(nc.scalar.copy, z_rows[0][:, :, HALF * c : HALF * (c + 1)], f"z_b0{c}") for c in range(2)
-        ]
-        nc.vector.tensor_copy(
-            out=wm_w[:].rearrange("p a (t m) -> p a m t", t=PACK),
-            in_=wm_raw[:].rearrange("p a (m t) -> p a m t", t=PACK),
-        )
-        nc.vector.tensor_copy(
-            out=wm_s[:].rearrange("p (t m) -> p t m", t=PACK),
-            in_=wm_sraw[:].rearrange("p (m t) -> p t m", t=PACK),
-        )
-        nc.vector.tensor_tensor(bo_faded[:], bo_sb, fader_sb, MULT)
-        for t in range(PACK):
-            add_direct(1, t)
-        woven1 = weave(nc.vector.tensor_copy, z_rows[1][:], "z_b10")
-        quantise(z_w[0][0][:], z_s[0][0][:], woven0[0])
-        quantise(z_w[1][0][:], z_s[1][0][:], woven1)
-        banks = open_y(0, 0)
-        close_y(0, 1, banks, ())
-        for t in range(PACK):
-            add_direct(2, t)
-        woven2 = weave(nc.vector.tensor_copy, z_rows[2][:], "z_b11")
-        quantise(z_w[0][1][:], z_s[0][1][:], woven0[1])
-        banks = open_y(1, 0)
-        quantise(z_w[1][1][:], z_s[1][1][:], woven2)
-        store_planes(0)
-        close_y(1, 1, banks, (3,))
-        store_planes(1)
-        for q in range(4):
+        close_mix(0, open_mix(0), on_vector=())
+        second = open_mix(1)
+        store_codes(0)
+        close_mix(1, second, on_vector=(PACK - 1,))
+        store_codes(1)
+        for q in range(P // QUAD):
             queue = nc.sync if q % 2 == 0 else nc.scalar
             queue.dma_start(
-                out=out_2[0, 4 * q : 4 * q + 4, :].bitcast(I32),
-                in_=y_s[32 * q : 32 * q + 4, :].bitcast(I32),
+                out=out_2[0, QUAD_ROWS * q : QUAD_ROWS * (q + 1), :].bitcast(I32),
+                in_=y_s[QUAD * q : QUAD * q + QUAD_ROWS, :].bitcast(I32),
             )

@@ -25,7 +25,9 @@ GROUP = 16
 QUAD = 32
 QUAD_ROWS = 4
 RUN = 4
-HALF = M // 2
+
+
+CHUNKS = ((0, 256), (256, 128), (384, 128))
 
 
 def tile_list_delay_tap_mixer_kernel(
@@ -35,17 +37,19 @@ def tile_list_delay_tap_mixer_kernel(
     nc = tc.nc
     with ExitStack() as ctx:
         held = ctx.enter_context(tc.tile_pool(name="held", bufs=1))
-        h_psum = ctx.enter_context(tc.psum_pool(name="h_psum", bufs=4))
-        d_psum = ctx.enter_context(tc.psum_pool(name="d_psum", bufs=4))
+        rings = [ctx.enter_context(tc.psum_pool(name=f"ring{i}", bufs=4)) for i in range(2)]
 
         def sbuf(shape, dtype, name, after=None):
             return held.tile(shape, dtype, name=name, tag=after or name, align_bytes=64)
 
+        def bank(ring, width):
+            return rings[ring].tile([P, width], F32, name="acc")
+
         def quantise(words, plane, woven):
             nc.vector.quantize_mx(out=words.bitcast(FP8X4), scales=plane, in_=woven)
 
-        def weave(copy, rows, name):
-            woven = sbuf([P, rows.shape[2], PACK], BF16, name)
+        def weave(copy, rows, name, after=None):
+            woven = sbuf([P, rows.shape[2], PACK], BF16, name, after)
             copy(
                 out=woven[:].rearrange("p (c i) t -> p c t i", i=RUN),
                 in_=rows.rearrange("p t (c i) -> p c t i", i=RUN),
@@ -61,9 +65,10 @@ def tile_list_delay_tap_mixer_kernel(
         w4_raw = [sbuf([P, 2, 2 * PASS], U8, f"w4_raw{b}") for b in range(2)]
         w4_sraw = sbuf([P, 2, H], U8, "w4_sraw")
         w4_s = [[sbuf([P, PASS], U8, f"w4_s{b}{a}") for a in range(2)] for b in range(2)]
+        w4_w = [[sbuf([P, 2 * PASS], U8, f"w4_w{b}{a}") for a in range(2)] for b in range(2)]
 
         for plane in (tab_s, w4_sraw, v_s[1]):
-            nc.vector.memset(plane[:].bitcast(I32), 0)
+            nc.gpsimd.memset(plane[:].bitcast(I32), 0)
 
         def load_w4(b):
             nc.sync.dma_start(
@@ -75,33 +80,36 @@ def tile_list_delay_tap_mixer_kernel(
             nc.sync.dma_start(out=tab_w[a][:], in_=tab_words[a].rearrange("p t i -> p (t i)").bitcast(I32))
 
         nc.sync.dma_start(list1[:], offs)
-        load_w4(0)
         for r in range(QUAD_ROWS):
             nc.sync.dma_start(
                 out=tab_s[r : P : QUAD // 2, :].bitcast(I32),
                 in_=tab_scales.rearrange("a (q r) c -> r q a c", r=QUAD_ROWS)[r].bitcast(I32),
             )
+        load_w4(0)
         load_table(0)
-        for q in range(P // QUAD):
+        for r in range(QUAD_ROWS):
             nc.sync.dma_start(
-                out=w4_sraw[QUAD * q : QUAD * q + QUAD_ROWS, :, :].bitcast(I32),
-                in_=w4_scales[:, QUAD_ROWS * q : QUAD_ROWS * (q + 1), :].rearrange("a r c -> r a c").bitcast(I32),
+                out=w4_sraw[r:P:QUAD, :, :].bitcast(I32),
+                in_=w4_scales.rearrange("a (q r) c -> r q a c", r=QUAD_ROWS)[r].bitcast(I32),
             )
         load_table(1)
         load_w4(1)
 
-        def deal_w4(b, after=None):
-            words = sbuf([P, 2, 2 * PASS], U8, f"w4_w{b}", after)
-            nc.vector.tensor_copy(
-                out=words[:].bitcast(U16).rearrange("p a (t m) -> p a t m", t=PACK),
-                in_=w4_raw[b][:].bitcast(U16).rearrange("p a (m t) -> p a t m", t=PACK),
+        def deal_w4(copy, b, a):
+            copy(
+                out=w4_w[b][a][:].bitcast(U16).rearrange("p (t m) -> p t m", t=PACK),
+                in_=w4_raw[b][:, a, :].bitcast(U16).rearrange("p (m t) -> p t m", t=PACK),
             )
-            return words
 
-        def gather_table(a):
-            for jh in range(2):
-                entries = list1[:, jh * BANK // GROUP : (jh + 1) * BANK // GROUP]
-                nc.vector.tensor_copy(v_w[a][jh][:], tab_w[a][:].bitcast(U32).indirect(entries))
+        def deal_w4_plane(b, a):
+            nc.gpsimd.tensor_copy(
+                out=w4_s[b][a][:].rearrange("p (t m) -> p t m", t=PACK),
+                in_=w4_sraw[:, a, PASS * b : PASS * (b + 1)].rearrange("p (m t) -> p t m", t=PACK),
+            )
+
+        def gather_table(a, jh):
+            entries = list1[:, jh * BANK // GROUP : (jh + 1) * BANK // GROUP]
+            nc.vector.tensor_copy(v_w[a][jh][:], tab_w[a][:].bitcast(U32).indirect(entries))
 
         def load_wd(b, after):
             rows = sbuf([P, PACK, PASS], F32, f"wd_raw{b}", after)
@@ -110,43 +118,27 @@ def tile_list_delay_tap_mixer_kernel(
             )
             return rows
 
-        w4_w = [deal_w4(0)]
         nc.vector.tensor_copy(v_s[0][:], tab_s[:].indirect(list1[:]))
         nc.sync.dma_start(
             out=v_s[1][0 : P - QUAD // 2, :].bitcast(I32), in_=v_s[0][QUAD // 2 : P, :].bitcast(I32)
         )
-        dry_raw = sbuf([P, PACK, M], F32, "dry_raw", "tab_s")
-        nc.sync.dma_start(out=dry_raw[:], in_=dry.rearrange("(p j) m -> p j m", j=PACK))
-        nc.sync.dma_start(list2[:], offs2)
+        deal_w4(nc.gpsimd.tensor_copy, 0, 0)
+        deal_w4(nc.gpsimd.tensor_copy, 0, 1)
         for b in range(2):
             for a in range(2):
-                nc.gpsimd.tensor_copy(
-                    out=w4_s[b][a][:].rearrange("p (t m) -> p t m", t=PACK),
-                    in_=w4_sraw[:, a, PASS * b : PASS * (b + 1)].rearrange("p (m t) -> p t m", t=PACK),
-                )
-        wgt_sb = sbuf([P, M], F32, "wgt_sb", "w4_sraw")
-        nc.sync.dma_start(out=wgt_sb[:], in_=wgt)
-        gather_table(0)
-        wd_raw = [load_wd(0, "tab_w0")]
-        gather_table(1)
-        w4_w.append(deal_w4(1, "tab_w1"))
-
-        dry_w = sbuf([P, M], U32, "dry_w")
-        dry_s = sbuf([P, M], U8, "dry_s")
-        dry_woven = weave(nc.vector.tensor_copy, dry_raw[:], "dry_woven")
-        wd_raw.append(load_wd(1, "tab_s"))
-        quantise(dry_w[:], dry_s[:], dry_woven)
-
-        wd_w = [sbuf([P, PASS], U32, f"wd_w{b}") for b in range(2)]
-        wd_s = [sbuf([P, PASS], U8, f"wd_s{b}") for b in range(2)]
-
-        def quantise_wd(b):
-            woven = sbuf([P, PACK, P, PACK], BF16, f"wd_woven{b}")
-            nc.scalar.copy(
-                out=woven[:].rearrange("p t m j -> p m j t"),
-                in_=wd_raw[b][:].rearrange("p j (m t) -> p m j t", t=PACK),
-            )
-            quantise(wd_w[b][:], wd_s[b][:], woven[:].rearrange("p t m j -> p (t m j)"))
+                deal_w4_plane(b, a)
+        deal_w4(nc.gpsimd.tensor_copy, 1, 0)
+        nc.sync.dma_start(list2[:], offs2)
+        wgt_tile = sbuf([P, M], F32, "wgt_sb", "tab_s")
+        wgt_sb = wgt_tile[:]
+        nc.sync.dma_start(out=wgt_sb, in_=wgt)
+        dry_raw = sbuf([P, PACK, M], F32, "dry_raw", "w4_raw0")
+        nc.sync.dma_start(out=dry_raw[:], in_=dry.rearrange("(p j) m -> p j m", j=PACK))
+        for a in range(2):
+            for jh in range(2):
+                gather_table(a, jh)
+        deal_w4(nc.vector.tensor_copy, 1, 1)
+        wd_raw = [load_wd(0, "tab_w0"), load_wd(1, "tab_w1")]
 
         vectors = sbuf([P, 3, 2 * PACK], F32, "vectors", "w4_raw1")
         gain_sb = vectors[:, 0, :]
@@ -158,94 +150,127 @@ def tile_list_delay_tap_mixer_kernel(
         nc.sync.dma_start(out=bo_sb, in_=bo.rearrange("(p t) -> p t", t=PACK))
         nc.sync.dma_start(out=fader_sb, in_=fader.rearrange("(p t) -> p t", t=PACK))
 
-        h_sb = [sbuf([P, S], F32, f"h_sb{s}") for s in range(2 * PACK)]
+        dry_w = sbuf([P, M], U32, "dry_w")
+        dry_s = sbuf([P, M], U8, "dry_s")
 
-        def make_h(*slices):
-            banks = [(s, jh, h_psum.tile([P, BANK], F32, name="acc")) for jh in range(2) for s in slices]
-            for a in range(2):
-                for s, jh, acc in banks:
-                    b, t = divmod(s, PACK)
-                    nc.tensor.matmul_mx(
-                        out=acc[:],
-                        lhsT=w4_w[b][:, a, 2 * P * t : 2 * P * (t + 1)].bitcast(FP4X4),
-                        lhsT_scale=w4_s[b][a][:, P * t : P * (t + 1)],
-                        rhs=v_w[a][jh][:].bitcast(FP8X4),
-                        rhs_scale=v_s[a][:, BANK * jh : BANK * (jh + 1)],
-                        start=(a == 0),
-                        stop=(a == 1),
-                    )
-                    if a == 1:
-                        nc.scalar.activation(out=h_sb[s][:, BANK * jh : BANK * (jh + 1)], in_=acc[:], func=ACT.Copy)
+        wd_w = [sbuf([P, PASS], U32, f"wd_w{b}") for b in range(2)]
+        wd_s = [sbuf([P, PASS], U8, f"wd_s{b}") for b in range(2)]
 
-        make_h(0, 1)
+        def round_wd(b):
+            woven = sbuf([P, PACK, P, PACK], BF16, f"wd_woven{b}")
+            nc.scalar.copy(
+                out=woven[:].rearrange("p t m j -> p m j t"),
+                in_=wd_raw[b][:].rearrange("p j (m t) -> p m j t", t=PACK),
+            )
+            return woven[:].rearrange("p t m j -> p (t m j)")
+
+        def direct(b):
+            banks = [bank(1 - b, M) for t in range(PACK)]
+            for t in range(PACK):
+                nc.tensor.matmul_mx(
+                    out=banks[t][:],
+                    lhsT=wd_w[b][:, P * t : P * (t + 1)].bitcast(FP8X4),
+                    lhsT_scale=wd_s[b][:, P * t : P * (t + 1)],
+                    rhs=dry_w[:].bitcast(FP8X4),
+                    rhs_scale=dry_s[:],
+                    start=True,
+                    stop=True,
+                )
+            return banks
+
+        h_sb = [sbuf([P, S], F32, f"h_sb{s}") for s in range(6)]
+
+        def h_pass(acc, s, jh, a):
+            b, t = divmod(s, PACK)
+            nc.tensor.matmul_mx(
+                out=acc[:],
+                lhsT=w4_w[b][a][:, 2 * P * t : 2 * P * (t + 1)].bitcast(FP4X4),
+                lhsT_scale=w4_s[b][a][:, P * t : P * (t + 1)],
+                rhs=v_w[a][jh][:].bitcast(FP8X4),
+                rhs_scale=v_s[a][:, BANK * jh : BANK * (jh + 1)],
+                start=(a == 0),
+                stop=(a == 1),
+            )
+
+        def h_out(acc, s, jh):
+            nc.scalar.activation(out=h_sb[s][:, BANK * jh : BANK * (jh + 1)], in_=acc[:], func=ACT.Copy)
+
+        def h_whole(s, jh):
+            acc = bank(0, BANK)
+            h_pass(acc, s, jh, 0)
+            h_pass(acc, s, jh, 1)
+            h_out(acc, s, jh)
+
+        order = [(0, 0), (1, 0), (0, 1), (1, 1)]
+        first = {key: bank(0, BANK) for key in order}
+        for s, jh in order:
+            h_pass(first[(s, jh)], s, jh, 0)
+        for s, jh in order:
+            h_pass(first[(s, jh)], s, jh, 1)
+            h_out(first[(s, jh)], s, jh)
         for s in range(2, 2 * PACK):
-            make_h(s)
+            if s == 6:
+                wd_woven0 = round_wd(0)
+                h_sb.append(sbuf([P, S], F32, "h_sb6", "tab_w0"))
+                h_sb.append(sbuf([P, S], F32, "h_sb7"))
+            for jh in range(2):
+                h_whole(s, jh)
 
         taps = [sbuf([P, PACK, M], F32, f"taps{b}") for b in range(2)]
         wet = [sbuf([P, PACK, M], F32, f"wet{b}") for b in range(2)]
         for s in range(2 * PACK):
             b, t = divmod(s, PACK)
-            nc.vector.tensor_tensor(taps[b][:, t, :], h_sb[s][:].indirect(list2[:]), wgt_sb[:], MULT)
+            nc.vector.tensor_tensor(taps[b][:, t, :], h_sb[s][:].indirect(list2[:]), wgt_sb, MULT)
+            if s == 0:
+                dry_woven = weave(nc.vector.tensor_copy, dry_raw[:], "dry_woven", "h_sb0")
+            if s == 1:
+                quantise(dry_w[:], dry_s[:], dry_woven)
+            if s == 5:
+                quantise(wd_w[0][:], wd_s[0][:], wd_woven0)
+                direct0 = direct(0)
 
-        def saturate(b):
-            for t in range(PACK):
-                nc.scalar.activation(out=wet[b][:, t, :], in_=taps[b][:, t, :], func=ACT.Tanh)
-
-        def sum_z(b, m0, width):
-            z_rows = sbuf([P, PACK, width], BF16, f"z_rows{b}_{m0}")
-            cols = slice(m0, m0 + width)
-            for t in range(PACK):
-                direct = d_psum.tile([P, width], F32, name="direct")
-                nc.tensor.matmul_mx(
-                    out=direct[:],
-                    lhsT=wd_w[b][:, P * t : P * (t + 1)].bitcast(FP8X4),
-                    lhsT_scale=wd_s[b][:, P * t : P * (t + 1)],
-                    rhs=dry_w[:, cols].bitcast(FP8X4),
-                    rhs_scale=dry_s[:, cols],
-                    start=True,
-                    stop=True,
-                )
-                s = PACK * b + t
-                nc.vector.scalar_tensor_tensor(
-                    out=z_rows[:, t, :], in0=wet[b][:, t, cols], scalar=gain_sb[:, s : s + 1], in1=direct[:],
-                    op0=MULT, op1=ADD,
-                )
-            return z_rows
-
-        quantise_wd(0)
-        wm_raw = sbuf([P, 2, N], I32, "wm_raw", "tab_w0")
+        wm_raw = sbuf([P, 2, N], I32, "wm_raw", "w4_raw0")
         nc.sync.dma_start(out=wm_raw[:], in_=wm_words.rearrange("a p c i -> p a (c i)").bitcast(I32))
-        wm_sraw = sbuf([P, N], U8, "wm_sraw", "v_w00")
+        wm_sraw = sbuf([P, N], U8, "wm_sraw", "w4_sraw")
         nc.gpsimd.memset(wm_sraw[:].bitcast(I32), 0)
         for q in range(P // QUAD):
             nc.sync.dma_start(
                 out=wm_sraw[QUAD * q : QUAD * q + 2 * QUAD_ROWS, :].bitcast(I32),
                 in_=wm_scales[:, QUAD_ROWS * q : QUAD_ROWS * (q + 1), :].bitcast(I32),
             )
-        saturate(0)
-        z_rows0 = sum_z(0, 0, M)
-        quantise_wd(1)
-        saturate(1)
-        z_woven0 = [
-            weave(nc.scalar.copy, z_rows0[:, :, HALF * c : HALF * (c + 1)], f"z_woven0{c}") for c in range(2)
-        ]
-
-        wm_w = sbuf([P, 2, N], I32, "wm_w")
-        wm_s = sbuf([P, N], U8, "wm_s")
+        wm_all = sbuf([P, 2 * N + N // PACK], I32, "wm_all", "h_sb7")
+        wm_w = wm_all[:, 0 : 2 * N].rearrange("p (a c) -> p a c", a=2)
+        wm_s = wm_all[:, 2 * N :].bitcast(U8)
         bo_faded = sbuf([P, PACK], F32, "bo_faded")
-        nc.vector.tensor_copy(
-            out=wm_w[:].rearrange("p a (t m) -> p a m t", t=PACK),
-            in_=wm_raw[:].rearrange("p a (m t) -> p a m t", t=PACK),
-        )
-        nc.vector.tensor_copy(
-            out=wm_s[:].rearrange("p (t m) -> p t m", t=PACK),
+        for a in range(2):
+            nc.gpsimd.tensor_copy(
+                out=wm_w[:, a, :].rearrange("p (t m) -> p t m", t=PACK),
+                in_=wm_raw[:, a, :].rearrange("p (m t) -> p t m", t=PACK),
+            )
+        nc.gpsimd.tensor_copy(
+            out=wm_s.rearrange("p (t m) -> p t m", t=PACK),
             in_=wm_sraw[:].rearrange("p (m t) -> p t m", t=PACK),
         )
         nc.vector.tensor_tensor(bo_faded[:], bo_sb, fader_sb, MULT)
 
-        z_w = [[sbuf([P, HALF], U32, f"z_w{b}{c}") for c in range(2)] for b in range(2)]
-        z_s = [[sbuf([P, HALF], U8, f"z_s{b}{c}") for c in range(2)] for b in range(2)]
-        y_rows = [sbuf([P, PACK, HALF], F32, f"y_rows{c}") for c in range(2)]
+        def saturate(b, rows, cols):
+            nc.scalar.activation(out=wet[b][:, rows, cols], in_=taps[b][:, rows, cols], func=ACT.Tanh)
+
+        def sum_z(b, banks, m0, width, z_rows=None, slices=range(PACK)):
+            if z_rows is None:
+                z_rows = sbuf([P, PACK, width], BF16, f"z_rows{b}_{m0}")
+            cols = slice(m0, m0 + width)
+            for t in slices:
+                s = PACK * b + t
+                nc.vector.scalar_tensor_tensor(
+                    out=z_rows[:, t, :], in0=wet[b][:, t, cols], scalar=gain_sb[:, s : s + 1], in1=banks[t][:, cols],
+                    op0=MULT, op1=ADD,
+                )
+            return z_rows
+
+        z_w = [sbuf([P, M], U32, f"z_w{b}") for b in range(2)]
+        z_s = [sbuf([P, M], U8, f"z_s{b}") for b in range(2)]
+        y_rows = [sbuf([P, PACK, w], F32, f"y_rows{c}") for c, (m0, w) in enumerate(CHUNKS)]
         y_w = sbuf([P, M], U32, "y_w")
         y_s = sbuf([P, M], U8, "y_s")
 
@@ -254,23 +279,42 @@ def tile_list_delay_tap_mixer_kernel(
                 out=acc[:],
                 lhsT=wm_w[:, b, P * t : P * (t + 1)].bitcast(FP8X4),
                 lhsT_scale=wm_s[QUAD_ROWS * b : P, P * t : P * (t + 1)],
-                rhs=z_w[b][c][:].bitcast(FP8X4),
-                rhs_scale=z_s[b][c][:],
+                rhs=z_w[b][:, chunk_cols(c)].bitcast(FP8X4),
+                rhs_scale=z_s[b][:, chunk_cols(c)],
                 start=(b == 0),
                 stop=(b == 1),
             )
 
+        y_woven = sbuf([P, M, PACK], BF16, "y_woven")
+
+        def weave_y(c, copy):
+            m0, w = CHUNKS[c]
+            copy(
+                out=y_woven[:, m0 : m0 + w, :].rearrange("p (c i) t -> p c t i", i=RUN),
+                in_=y_rows[c][:].rearrange("p t (c i) -> p c t i", i=RUN),
+            )
+
+        def store_codes(m0, w):
+            cols = slice(m0, m0 + w)
+            quantise(y_w[:, cols], y_s[:, cols], y_woven[:, cols, :].rearrange("p m t -> p (m t)"))
+            nc.sync.dma_start(
+                out=out_1[0].rearrange("p m t -> p (m t)").bitcast(I32)[:, cols], in_=y_w[:, cols].bitcast(I32)
+            )
+
+        def chunk_cols(c):
+            return slice(CHUNKS[c][0], CHUNKS[c][0] + CHUNKS[c][1])
+
+        def quantise_z(b, cols, woven):
+            quantise(z_w[b][:, cols], z_s[b][:, cols], woven)
+
         def open_mix(c):
-            z_rows1 = sum_z(1, HALF * c, HALF)
-            z_woven1 = weave(nc.vector.tensor_copy, z_rows1[:], f"z_woven1{c}")
-            quantise(z_w[0][c][:], z_s[0][c][:], z_woven0[c])
-            banks = [h_psum.tile([P, HALF], F32, name="acc") for t in range(PACK)]
+            banks = [bank(1 - c % 2, CHUNKS[c][1]) for t in range(PACK)]
             for t in range(PACK):
                 mix_pass(banks[t], c, t, 0)
-            quantise(z_w[1][c][:], z_s[1][c][:], z_woven1)
             return banks
 
         def close_mix(c, banks, on_vector):
+            m0, w = CHUNKS[c]
             for t in range(PACK):
                 mix_pass(banks[t], c, t, 1)
                 if t in on_vector:
@@ -283,21 +327,41 @@ def tile_list_delay_tap_mixer_kernel(
                         out=y_rows[c][:, t, :], in_=banks[t][:], func=ACT.Identity,
                         scale=fader_sb[:, t : t + 1], bias=bo_faded[:, t : t + 1],
                     )
-            cols = slice(HALF * c, HALF * (c + 1))
-            nc.sync.dma_start(out=out_0[:, cols].rearrange("(p t) m -> p t m", t=PACK), in_=y_rows[c][:])
+            nc.sync.dma_start(out=out_0[:, m0 : m0 + w].rearrange("(p t) m -> p t m", t=PACK), in_=y_rows[c][:])
 
-        def store_codes(c):
-            cols = slice(HALF * c, HALF * (c + 1))
-            quantise(y_w[:, cols], y_s[:, cols], weave(nc.vector.tensor_copy, y_rows[c][:], f"y_woven{c}"))
-            nc.sync.dma_start(
-                out=out_1[0].rearrange("p m t -> p (m t)").bitcast(I32)[:, cols], in_=y_w[:, cols].bitcast(I32)
-            )
+        saturate(0, slice(0, 2), slice(0, M))
+        z_rows0 = sum_z(0, direct0, 0, M, None, (0, 1))
+        quantise(wd_w[1][:], wd_s[1][:], round_wd(1))
+        direct1 = direct(1)
+        saturate(0, slice(2, 4), slice(0, M))
+        sum_z(0, direct0, 0, M, z_rows0, (2, 3))
+        lo, hi = slice(0, 256), slice(256, 512)
+        saturate(1, slice(0, PACK), lo)
+        z0a = weave(nc.vector.tensor_copy, z_rows0[:, :, lo], "z_woven00")
+        saturate(1, slice(0, PACK), hi)
+        z0b = weave(nc.scalar.copy, z_rows0[:, :, hi], "z_woven01")
 
-        close_mix(0, open_mix(0), on_vector=())
-        second = open_mix(1)
-        store_codes(0)
-        close_mix(1, second, on_vector=(PACK - 1,))
-        store_codes(1)
+        rows_a = sum_z(1, direct1, 0, 256)
+        z1a = weave(nc.vector.tensor_copy, rows_a[:], "z_woven10")
+        quantise_z(0, lo, z0a)
+        mix_a = open_mix(0)
+        quantise_z(1, lo, z1a)
+        close_mix(0, mix_a, ())
+        rows_b = sum_z(1, direct1, 256, 256)
+        z1b = weave(nc.vector.tensor_copy, rows_b[:, :, 0:128], "z_woven11")
+        quantise_z(0, hi, z0b)
+        mix_b = open_mix(1)
+        quantise_z(1, chunk_cols(1), z1b)
+        close_mix(1, mix_b, ())
+        z1c = weave(nc.vector.tensor_copy, rows_b[:, :, 128:256], "z_woven12")
+        weave_y(0, nc.vector.tensor_copy)
+        mix_c = open_mix(2)
+        quantise_z(1, chunk_cols(2), z1c)
+        close_mix(2, mix_c, ())
+        store_codes(0, 256)
+        weave_y(1, nc.vector.tensor_copy)
+        weave_y(2, nc.vector.tensor_copy)
+        store_codes(256, 256)
         for q in range(P // QUAD):
             queue = nc.sync if q % 2 == 0 else nc.scalar
             queue.dma_start(

@@ -129,16 +129,19 @@ def tile_list_delay_tap_mixer_kernel(
                 deal_w4_plane(b, a)
         deal_w4(nc.gpsimd.tensor_copy, 1, 0)
         nc.sync.dma_start(list2[:], offs2)
-        wgt_tile = sbuf([P, M], F32, "wgt_sb", "tab_s")
-        wgt_sb = wgt_tile[:]
-        nc.sync.dma_start(out=wgt_sb, in_=wgt)
-        dry_raw = sbuf([P, PACK, M], F32, "dry_raw", "w4_raw0")
-        nc.sync.dma_start(out=dry_raw[:], in_=dry.rearrange("(p j) m -> p j m", j=PACK))
         for a in range(2):
             for jh in range(2):
                 gather_table(a, jh)
+        dry_rows = dry.rearrange("(p j) m -> p j m", j=PACK)
+        dry_lo = sbuf([P, PACK, M // 2], F32, "dry_lo", "tab_s")
+        nc.sync.dma_start(out=dry_lo[:], in_=dry_rows[:, :, 0 : M // 2])
+        dry_hi = sbuf([P, PACK, M // 2], F32, "dry_hi", "w4_raw0")
+        nc.sync.dma_start(out=dry_hi[:], in_=dry_rows[:, :, M // 2 : M])
+        wgt_tile = sbuf([P, M], F32, "wgt_sb", "tab_w0")
+        wgt_sb = wgt_tile[:]
+        nc.sync.dma_start(out=wgt_sb, in_=wgt)
         deal_w4(nc.vector.tensor_copy, 1, 1)
-        wd_raw = [load_wd(0, "tab_w0"), load_wd(1, "tab_w1")]
+        wd_raw = [load_wd(0, "tab_w1"), load_wd(1, "tab_s")]
 
         vectors = sbuf([P, 3, 2 * PACK], F32, "vectors", "w4_raw1")
         gain_sb = vectors[:, 0, :]
@@ -152,6 +155,16 @@ def tile_list_delay_tap_mixer_kernel(
 
         dry_w = sbuf([P, M], U32, "dry_w")
         dry_s = sbuf([P, M], U8, "dry_s")
+        dry_woven = sbuf([P, M, PACK], BF16, "dry_woven")
+
+        def weave_dry(rows, cols):
+            nc.vector.tensor_copy(
+                out=dry_woven[:, cols, :].rearrange("p (c i) t -> p c t i", i=RUN),
+                in_=rows.rearrange("p t (c i) -> p c t i", i=RUN),
+            )
+
+        weave_dry(dry_lo[:], slice(0, M // 2))
+        weave_dry(dry_hi[:], slice(M // 2, M))
 
         wd_w = [sbuf([P, PASS], U32, f"wd_w{b}") for b in range(2)]
         wd_s = [sbuf([P, PASS], U8, f"wd_s{b}") for b in range(2)]
@@ -211,7 +224,7 @@ def tile_list_delay_tap_mixer_kernel(
         for s in range(2, 2 * PACK):
             if s == 6:
                 wd_woven0 = round_wd(0)
-                h_sb.append(sbuf([P, S], F32, "h_sb6", "tab_w0"))
+                h_sb.append(sbuf([P, S], F32, "h_sb6", "tab_w1"))
                 h_sb.append(sbuf([P, S], F32, "h_sb7"))
             for jh in range(2):
                 h_whole(s, jh)
@@ -222,9 +235,7 @@ def tile_list_delay_tap_mixer_kernel(
             b, t = divmod(s, PACK)
             nc.vector.tensor_tensor(taps[b][:, t, :], h_sb[s][:].indirect(list2[:]), wgt_sb, MULT)
             if s == 0:
-                dry_woven = weave(nc.vector.tensor_copy, dry_raw[:], "dry_woven", "h_sb0")
-            if s == 1:
-                quantise(dry_w[:], dry_s[:], dry_woven)
+                quantise(dry_w[:], dry_s[:], dry_woven[:].rearrange("p m t -> p (m t)"))
             if s == 5:
                 quantise(wd_w[0][:], wd_s[0][:], wd_woven0)
                 direct0 = direct(0)

@@ -27,6 +27,7 @@ QUAD_ROWS = 4
 RUN = 4
 
 
+HALF = M // 2
 CHUNKS = ((0, 256), (256, 128), (384, 128))
 
 
@@ -37,79 +38,111 @@ def tile_list_delay_tap_mixer_kernel(
     nc = tc.nc
     with ExitStack() as ctx:
         held = ctx.enter_context(tc.tile_pool(name="held", bufs=1))
-        rings = [ctx.enter_context(tc.psum_pool(name=f"ring{i}", bufs=4)) for i in range(2)]
+        psum = ctx.enter_context(tc.psum_pool(name="psum", bufs=1))
 
         def sbuf(shape, dtype, name, after=None):
             return held.tile(shape, dtype, name=name, tag=after or name, align_bytes=64)
 
-        def bank(ring, width):
-            return rings[ring].tile([P, width], F32, name="acc")
+        def bank(k, shape):
+            return psum.tile(shape, F32, name=f"bank{k}", tag=f"bank{k}")
 
         def quantise(words, plane, woven):
             nc.vector.quantize_mx(out=words.bitcast(FP8X4), scales=plane, in_=woven)
 
-        def weave(copy, rows, name, after=None):
-            woven = sbuf([P, rows.shape[2], PACK], BF16, name, after)
+        def weave_into(copy, woven, rows):
             copy(
-                out=woven[:].rearrange("p (c i) t -> p c t i", i=RUN),
+                out=woven.rearrange("p (c i) t -> p c t i", i=RUN),
                 in_=rows.rearrange("p t (c i) -> p c t i", i=RUN),
             )
+
+        def weave(copy, rows, name, after=None):
+            woven = sbuf([P, rows.shape[2], PACK], BF16, name, after)
+            weave_into(copy, woven[:], rows)
             return woven[:].rearrange("p m t -> p (m t)")
+
+        def deal(copy, dealt, raw):
+            copy(out=dealt, in_=raw.rearrange("p (m t) -> p t m", t=PACK))
 
         list1 = held.tile([P, S // GROUP], U16, name="list1")
         list2 = held.tile([P, M // GROUP], U16, name="list2")
         tab_w = [sbuf([P, T], I32, f"tab_w{a}") for a in range(2)]
         tab_s = sbuf([P, T], U8, "tab_s")
+        picked_s = sbuf([P, S], U8, "picked_s")
         v_w = [[sbuf([P, BANK], U32, f"v_w{a}{jh}") for jh in range(2)] for a in range(2)]
-        v_s = [sbuf([P, S], U8, f"v_s{a}") for a in range(2)]
-        w4_raw = [sbuf([P, 2, 2 * PASS], U8, f"w4_raw{b}") for b in range(2)]
+        v_s = sbuf([P, 2, S], U8, "v_s")
         w4_sraw = sbuf([P, 2, H], U8, "w4_sraw")
         w4_s = [[sbuf([P, PASS], U8, f"w4_s{b}{a}") for a in range(2)] for b in range(2)]
         w4_w = [[sbuf([P, 2 * PASS], U8, f"w4_w{b}{a}") for a in range(2)] for b in range(2)]
+        rows0 = P - QUAD
 
-        for plane in (tab_s, w4_sraw, v_s[1]):
-            nc.gpsimd.memset(plane[:].bitcast(I32), 0)
+        nc.gpsimd.memset(w4_sraw[:].bitcast(I32), 0)
+        nc.vector.memset(tab_s[0:rows0, :].bitcast(I32), 0)
+        nc.gpsimd.memset(v_s[:].bitcast(I32), 0)
 
-        def load_w4(b):
+        def load_w4(b, after=None):
+            raw = sbuf([P, 2, 2 * PASS], U8, f"w4_raw{b}", after)
             nc.sync.dma_start(
-                out=w4_raw[b][:].bitcast(I32),
+                out=raw[:].bitcast(I32),
                 in_=w4_words[:, :, 2 * PASS * b : 2 * PASS * (b + 1)].rearrange("a p c -> p a c").bitcast(I32),
             )
+            return raw
 
         def load_table(a):
             nc.sync.dma_start(out=tab_w[a][:], in_=tab_words[a].rearrange("p t i -> p (t i)").bitcast(I32))
 
         nc.sync.dma_start(list1[:], offs)
-        for r in range(QUAD_ROWS):
-            nc.sync.dma_start(
-                out=tab_s[r : P : QUAD // 2, :].bitcast(I32),
-                in_=tab_scales.rearrange("a (q r) c -> r q a c", r=QUAD_ROWS)[r].bitcast(I32),
-            )
-        load_w4(0)
+        nc.sync.dma_start(
+            out=tab_s[rows0:P, :].bitcast(I32), in_=tab_scales.rearrange("a q c -> q a c").bitcast(I32)
+        )
         load_table(0)
+        w4_raw = [load_w4(0)]
         for r in range(QUAD_ROWS):
             nc.sync.dma_start(
                 out=w4_sraw[r:P:QUAD, :, :].bitcast(I32),
                 in_=w4_scales.rearrange("a (q r) c -> r q a c", r=QUAD_ROWS)[r].bitcast(I32),
             )
         load_table(1)
-        load_w4(1)
+        nc.sync.dma_start(list2[:], offs2)
+
+        nc.vector.tensor_copy(picked_s[:], tab_s[:].indirect(list1[:]))
+        for q in range(P // QUAD):
+            first = rows0 + 2 * QUAD_ROWS * q
+            nc.sync.dma_start(
+                out=v_s[QUAD * q : QUAD * q + QUAD_ROWS, :, :].bitcast(I32),
+                in_=picked_s[first : first + 2 * QUAD_ROWS, :].bitcast(I32),
+            )
+        w4_raw.append(load_w4(1, "tab_s"))
 
         def deal_w4(copy, b, a):
-            copy(
-                out=w4_w[b][a][:].bitcast(U16).rearrange("p (t m) -> p t m", t=PACK),
-                in_=w4_raw[b][:, a, :].bitcast(U16).rearrange("p (m t) -> p t m", t=PACK),
-            )
+            deal(copy, w4_w[b][a][:].bitcast(U16).rearrange("p (t m) -> p t m", t=PACK), w4_raw[b][:, a, :].bitcast(U16))
 
         def deal_w4_plane(b, a):
-            nc.gpsimd.tensor_copy(
-                out=w4_s[b][a][:].rearrange("p (t m) -> p t m", t=PACK),
-                in_=w4_sraw[:, a, PASS * b : PASS * (b + 1)].rearrange("p (m t) -> p t m", t=PACK),
+            deal(
+                nc.gpsimd.tensor_copy,
+                w4_s[b][a][:].rearrange("p (t m) -> p t m", t=PACK),
+                w4_sraw[:, a, PASS * b : PASS * (b + 1)],
             )
 
-        def gather_table(a, jh):
-            entries = list1[:, jh * BANK // GROUP : (jh + 1) * BANK // GROUP]
-            nc.vector.tensor_copy(v_w[a][jh][:], tab_w[a][:].bitcast(U32).indirect(entries))
+        for a in range(2):
+            deal_w4(nc.scalar.copy, 0, a)
+        for b in range(2):
+            for a in range(2):
+                deal_w4_plane(b, a)
+        deal_w4(nc.scalar.copy, 1, 0)
+        deal_w4(nc.gpsimd.tensor_copy, 1, 1)
+
+        for a in range(2):
+            for jh in range(2):
+                entries = list1[:, jh * BANK // GROUP : (jh + 1) * BANK // GROUP]
+                nc.vector.tensor_copy(v_w[a][jh][:], tab_w[a][:].bitcast(U32).indirect(entries))
+
+        dry_rows = dry.rearrange("(p j) m -> p j m", j=PACK)
+        dry_lo = sbuf([P, PACK, HALF], F32, "dry_lo", "picked_s")
+        nc.sync.dma_start(out=dry_lo[:], in_=dry_rows[:, :, 0:HALF])
+        dry_hi = sbuf([P, PACK, HALF], F32, "dry_hi", "w4_raw0")
+        nc.sync.dma_start(out=dry_hi[:], in_=dry_rows[:, :, HALF:M])
+        wgt_sb = sbuf([P, M], F32, "wgt_sb", "tab_w0")
+        nc.sync.dma_start(out=wgt_sb[:], in_=wgt)
 
         def load_wd(b, after):
             rows = sbuf([P, PACK, PASS], F32, f"wd_raw{b}", after)
@@ -118,32 +151,9 @@ def tile_list_delay_tap_mixer_kernel(
             )
             return rows
 
-        nc.vector.tensor_copy(v_s[0][:], tab_s[:].indirect(list1[:]))
-        nc.sync.dma_start(
-            out=v_s[1][0 : P - QUAD // 2, :].bitcast(I32), in_=v_s[0][QUAD // 2 : P, :].bitcast(I32)
-        )
-        deal_w4(nc.gpsimd.tensor_copy, 0, 0)
-        deal_w4(nc.gpsimd.tensor_copy, 0, 1)
-        for b in range(2):
-            for a in range(2):
-                deal_w4_plane(b, a)
-        deal_w4(nc.gpsimd.tensor_copy, 1, 0)
-        nc.sync.dma_start(list2[:], offs2)
-        for a in range(2):
-            for jh in range(2):
-                gather_table(a, jh)
-        dry_rows = dry.rearrange("(p j) m -> p j m", j=PACK)
-        dry_lo = sbuf([P, PACK, M // 2], F32, "dry_lo", "tab_s")
-        nc.sync.dma_start(out=dry_lo[:], in_=dry_rows[:, :, 0 : M // 2])
-        dry_hi = sbuf([P, PACK, M // 2], F32, "dry_hi", "w4_raw0")
-        nc.sync.dma_start(out=dry_hi[:], in_=dry_rows[:, :, M // 2 : M])
-        wgt_tile = sbuf([P, M], F32, "wgt_sb", "tab_w0")
-        wgt_sb = wgt_tile[:]
-        nc.sync.dma_start(out=wgt_sb, in_=wgt)
-        deal_w4(nc.vector.tensor_copy, 1, 1)
-        wd_raw = [load_wd(0, "tab_w1"), load_wd(1, "tab_s")]
+        wd_raw = [load_wd(0, "tab_w1"), load_wd(1, "picked_s")]
 
-        vectors = sbuf([P, 3, 2 * PACK], F32, "vectors", "w4_raw1")
+        vectors = sbuf([P, 3, 2 * PACK], F32, "vectors", "tab_s")
         gain_sb = vectors[:, 0, :]
         bo_sb = vectors[:, 1, 0:PACK]
         fader_sb = vectors[:, 2, 0:PACK]
@@ -156,15 +166,8 @@ def tile_list_delay_tap_mixer_kernel(
         dry_w = sbuf([P, M], U32, "dry_w")
         dry_s = sbuf([P, M], U8, "dry_s")
         dry_woven = sbuf([P, M, PACK], BF16, "dry_woven")
-
-        def weave_dry(rows, cols):
-            nc.vector.tensor_copy(
-                out=dry_woven[:, cols, :].rearrange("p (c i) t -> p c t i", i=RUN),
-                in_=rows.rearrange("p t (c i) -> p c t i", i=RUN),
-            )
-
-        weave_dry(dry_lo[:], slice(0, M // 2))
-        weave_dry(dry_hi[:], slice(M // 2, M))
+        weave_into(nc.vector.tensor_copy, dry_woven[:, 0:HALF, :], dry_lo[:])
+        weave_into(nc.vector.tensor_copy, dry_woven[:, HALF:M, :], dry_hi[:])
 
         wd_w = [sbuf([P, PASS], U32, f"wd_w{b}") for b in range(2)]
         wd_s = [sbuf([P, PASS], U8, f"wd_s{b}") for b in range(2)]
@@ -177,19 +180,25 @@ def tile_list_delay_tap_mixer_kernel(
             )
             return woven[:].rearrange("p t m j -> p (t m j)")
 
-        def direct(b):
-            banks = [bank(1 - b, M) for t in range(PACK)]
-            for t in range(PACK):
-                nc.tensor.matmul_mx(
-                    out=banks[t][:],
-                    lhsT=wd_w[b][:, P * t : P * (t + 1)].bitcast(FP8X4),
-                    lhsT_scale=wd_s[b][:, P * t : P * (t + 1)],
-                    rhs=dry_w[:].bitcast(FP8X4),
-                    rhs_scale=dry_s[:],
-                    start=True,
-                    stop=True,
-                )
-            return banks
+        def half_cols(x):
+            return slice(HALF * x, HALF * (x + 1))
+
+        def direct(b, first_bank):
+            sums = []
+            for x in range(2):
+                pairs = [bank(first_bank + 2 * x + u, [P, 2, HALF]) for u in range(2)]
+                for t in range(PACK):
+                    nc.tensor.matmul_mx(
+                        out=pairs[t // 2][:, t % 2, :],
+                        lhsT=wd_w[b][:, P * t : P * (t + 1)].bitcast(FP8X4),
+                        lhsT_scale=wd_s[b][:, P * t : P * (t + 1)],
+                        rhs=dry_w[:, half_cols(x)].bitcast(FP8X4),
+                        rhs_scale=dry_s[:, half_cols(x)],
+                        start=True,
+                        stop=True,
+                    )
+                sums.append([pairs[t // 2][:, t % 2, :] for t in range(PACK)])
+            return sums
 
         h_sb = [sbuf([P, S], F32, f"h_sb{s}") for s in range(6)]
 
@@ -200,47 +209,31 @@ def tile_list_delay_tap_mixer_kernel(
                 lhsT=w4_w[b][a][:, 2 * P * t : 2 * P * (t + 1)].bitcast(FP4X4),
                 lhsT_scale=w4_s[b][a][:, P * t : P * (t + 1)],
                 rhs=v_w[a][jh][:].bitcast(FP8X4),
-                rhs_scale=v_s[a][:, BANK * jh : BANK * (jh + 1)],
+                rhs_scale=v_s[:, a, BANK * jh : BANK * (jh + 1)],
                 start=(a == 0),
                 stop=(a == 1),
             )
+            if a == 1:
+                nc.scalar.activation(out=h_sb[s][:, BANK * jh : BANK * (jh + 1)], in_=acc[:], func=ACT.Copy)
 
-        def h_out(acc, s, jh):
-            nc.scalar.activation(out=h_sb[s][:, BANK * jh : BANK * (jh + 1)], in_=acc[:], func=ACT.Copy)
-
-        def h_whole(s, jh):
-            acc = bank(0, BANK)
-            h_pass(acc, s, jh, 0)
-            h_pass(acc, s, jh, 1)
-            h_out(acc, s, jh)
-
-        order = [(0, 0), (1, 0), (0, 1), (1, 1)]
-        first = {key: bank(0, BANK) for key in order}
-        for s, jh in order:
-            h_pass(first[(s, jh)], s, jh, 0)
-        for s, jh in order:
-            h_pass(first[(s, jh)], s, jh, 1)
-            h_out(first[(s, jh)], s, jh)
-        for s in range(2, 2 * PACK):
-            if s == 6:
+        early = [bank(k, [P, BANK]) for k in range(3)]
+        h_pass(early[0], 0, 0, 0)
+        h_pass(early[1], 0, 1, 0)
+        h_pass(early[0], 0, 0, 1)
+        h_pass(early[2], 1, 0, 0)
+        h_pass(early[2], 1, 0, 1)
+        h_pass(early[1], 0, 1, 1)
+        for k in range(3, 4 * PACK):
+            s, jh = divmod(k, 2)
+            if k == 12:
                 wd_woven0 = round_wd(0)
                 h_sb.append(sbuf([P, S], F32, "h_sb6", "tab_w1"))
                 h_sb.append(sbuf([P, S], F32, "h_sb7"))
-            for jh in range(2):
-                h_whole(s, jh)
+            acc = bank(k % 4, [P, BANK])
+            for a in range(2):
+                h_pass(acc, s, jh, a)
 
-        taps = [sbuf([P, PACK, M], F32, f"taps{b}") for b in range(2)]
-        wet = [sbuf([P, PACK, M], F32, f"wet{b}") for b in range(2)]
-        for s in range(2 * PACK):
-            b, t = divmod(s, PACK)
-            nc.vector.tensor_tensor(taps[b][:, t, :], h_sb[s][:].indirect(list2[:]), wgt_sb, MULT)
-            if s == 0:
-                quantise(dry_w[:], dry_s[:], dry_woven[:].rearrange("p m t -> p (m t)"))
-            if s == 5:
-                quantise(wd_w[0][:], wd_s[0][:], wd_woven0)
-                direct0 = direct(0)
-
-        wm_raw = sbuf([P, 2, N], I32, "wm_raw", "w4_raw0")
+        wm_raw = sbuf([P, 2, N], I32, "wm_raw", "w4_w00")
         nc.sync.dma_start(out=wm_raw[:], in_=wm_words.rearrange("a p c i -> p a (c i)").bitcast(I32))
         wm_sraw = sbuf([P, N], U8, "wm_sraw", "w4_sraw")
         nc.gpsimd.memset(wm_sraw[:].bitcast(I32), 0)
@@ -249,46 +242,67 @@ def tile_list_delay_tap_mixer_kernel(
                 out=wm_sraw[QUAD * q : QUAD * q + 2 * QUAD_ROWS, :].bitcast(I32),
                 in_=wm_scales[:, QUAD_ROWS * q : QUAD_ROWS * (q + 1), :].bitcast(I32),
             )
-        wm_all = sbuf([P, 2 * N + N // PACK], I32, "wm_all", "h_sb7")
-        wm_w = wm_all[:, 0 : 2 * N].rearrange("p (a c) -> p a c", a=2)
-        wm_s = wm_all[:, 2 * N :].bitcast(U8)
-        bo_faded = sbuf([P, PACK], F32, "bo_faded")
-        for a in range(2):
-            nc.gpsimd.tensor_copy(
-                out=wm_w[:, a, :].rearrange("p (t m) -> p t m", t=PACK),
-                in_=wm_raw[:, a, :].rearrange("p (m t) -> p t m", t=PACK),
-            )
-        nc.gpsimd.tensor_copy(
-            out=wm_s.rearrange("p (t m) -> p t m", t=PACK),
-            in_=wm_sraw[:].rearrange("p (m t) -> p t m", t=PACK),
-        )
+
+        taps = [sbuf([P, PACK, M], F32, "taps0", "w4_raw0"), sbuf([P, PACK, M], F32, "taps1")]
+        wet = [sbuf([P, PACK, M], F32, f"wet{b}") for b in range(2)]
+        for s in range(2 * PACK):
+            b, t = divmod(s, PACK)
+            nc.vector.tensor_tensor(taps[b][:, t, :], h_sb[s][:].indirect(list2[:]), wgt_sb[:], MULT)
+            if s == 0:
+                quantise(dry_w[:], dry_s[:], dry_woven[:].rearrange("p m t -> p (m t)"))
+            if s == 5:
+                quantise(wd_w[0][:], wd_s[0][:], wd_woven0)
+                direct0 = direct(0, 4)
+        bo_faded = sbuf([P, PACK], F32, "bo_faded", "h_sb4")
         nc.vector.tensor_tensor(bo_faded[:], bo_sb, fader_sb, MULT)
 
-        def saturate(b, rows, cols):
-            nc.scalar.activation(out=wet[b][:, rows, cols], in_=taps[b][:, rows, cols], func=ACT.Tanh)
+        wm_s = sbuf([P, N], U8, "wm_s", "h_sb7")
+        deal(nc.gpsimd.tensor_copy, wm_s[:].rearrange("p (t m) -> p t m", t=PACK), wm_sraw[:])
 
-        def sum_z(b, banks, m0, width, z_rows=None, slices=range(PACK)):
-            if z_rows is None:
-                z_rows = sbuf([P, PACK, width], BF16, f"z_rows{b}_{m0}")
-            cols = slice(m0, m0 + width)
-            for t in slices:
+        def saturate(b, x):
+            nc.scalar.activation(out=wet[b][:, :, half_cols(x)], in_=taps[b][:, :, half_cols(x)], func=ACT.Tanh)
+
+        def sum_z(b, x, sums):
+            z_rows = sbuf([P, PACK, HALF], BF16, f"z_rows{b}{x}")
+            for t in range(PACK):
                 s = PACK * b + t
                 nc.vector.scalar_tensor_tensor(
-                    out=z_rows[:, t, :], in0=wet[b][:, t, cols], scalar=gain_sb[:, s : s + 1], in1=banks[t][:, cols],
+                    out=z_rows[:, t, :], in0=wet[b][:, t, half_cols(x)], scalar=gain_sb[:, s : s + 1], in1=sums[x][t],
                     op0=MULT, op1=ADD,
                 )
             return z_rows
 
         z_w = [sbuf([P, M], U32, f"z_w{b}") for b in range(2)]
         z_s = [sbuf([P, M], U8, f"z_s{b}") for b in range(2)]
+
+        def quantise_z(b, cols, woven):
+            quantise(z_w[b][:, cols], z_s[b][:, cols], woven)
+
+        saturate(0, 0)
+        z00 = weave(nc.vector.tensor_copy, sum_z(0, 0, direct0)[:], "z_woven00")
+        quantise(wd_w[1][:], wd_s[1][:], round_wd(1))
+        direct1 = direct(1, 0)
+        wm_cols = wm_raw[:].rearrange("p a (m t) -> p a t m", t=PACK)
+        wm_first = sbuf([P, 2, P], I32, "wm_first", "wd_woven1")
+        nc.vector.tensor_copy(out=wm_first[:], in_=wm_cols[:, 0, 0:2, :])
+        quantise_z(0, half_cols(0), z00)
+        wm_rest = sbuf([P, 6, P], I32, "wm_rest", "z_woven00")
+        nc.gpsimd.tensor_copy(out=wm_rest[:, 0:2, :], in_=wm_cols[:, 0, 2:4, :])
+        nc.gpsimd.tensor_copy(out=wm_rest[:, 2:6, :], in_=wm_cols[:, 1, :, :])
+        wm_w = [wm_first[:, 0, :], wm_first[:, 1, :]] + [wm_rest[:, i, :] for i in range(6)]
+
         y_rows = [sbuf([P, PACK, w], F32, f"y_rows{c}") for c, (m0, w) in enumerate(CHUNKS)]
+        y_woven = sbuf([P, M, PACK], BF16, "y_woven")
         y_w = sbuf([P, M], U32, "y_w")
         y_s = sbuf([P, M], U8, "y_s")
+
+        def chunk_cols(c):
+            return slice(CHUNKS[c][0], CHUNKS[c][0] + CHUNKS[c][1])
 
         def mix_pass(acc, c, t, b):
             nc.tensor.matmul_mx(
                 out=acc[:],
-                lhsT=wm_w[:, b, P * t : P * (t + 1)].bitcast(FP8X4),
+                lhsT=wm_w[PACK * b + t].bitcast(FP8X4),
                 lhsT_scale=wm_s[QUAD_ROWS * b : P, P * t : P * (t + 1)],
                 rhs=z_w[b][:, chunk_cols(c)].bitcast(FP8X4),
                 rhs_scale=z_s[b][:, chunk_cols(c)],
@@ -296,83 +310,63 @@ def tile_list_delay_tap_mixer_kernel(
                 stop=(b == 1),
             )
 
-        y_woven = sbuf([P, M, PACK], BF16, "y_woven")
-
-        def weave_y(c, copy):
-            m0, w = CHUNKS[c]
-            copy(
-                out=y_woven[:, m0 : m0 + w, :].rearrange("p (c i) t -> p c t i", i=RUN),
-                in_=y_rows[c][:].rearrange("p t (c i) -> p c t i", i=RUN),
-            )
-
-        def store_codes(m0, w):
-            cols = slice(m0, m0 + w)
-            quantise(y_w[:, cols], y_s[:, cols], y_woven[:, cols, :].rearrange("p m t -> p (m t)"))
-            nc.sync.dma_start(
-                out=out_1[0].rearrange("p m t -> p (m t)").bitcast(I32)[:, cols], in_=y_w[:, cols].bitcast(I32)
-            )
-
-        def chunk_cols(c):
-            return slice(CHUNKS[c][0], CHUNKS[c][0] + CHUNKS[c][1])
-
-        def quantise_z(b, cols, woven):
-            quantise(z_w[b][:, cols], z_s[b][:, cols], woven)
-
-        def open_mix(c):
-            banks = [bank(1 - c % 2, CHUNKS[c][1]) for t in range(PACK)]
+        def open_mix(c, free):
+            banks = [bank(k, [P, CHUNKS[c][1]]) for k in free]
             for t in range(PACK):
                 mix_pass(banks[t], c, t, 0)
             return banks
 
-        def close_mix(c, banks, on_vector):
-            m0, w = CHUNKS[c]
+        def close_mix(c, banks, parts):
+            out_rows = out_0[:, chunk_cols(c)].rearrange("(p t) m -> p t m", t=PACK)
+            step = PACK // parts
             for t in range(PACK):
                 mix_pass(banks[t], c, t, 1)
-                if t in on_vector:
-                    nc.vector.tensor_scalar(
-                        out=y_rows[c][:, t, :], in0=banks[t][:], scalar1=bo_sb[:, t : t + 1],
-                        scalar2=fader_sb[:, t : t + 1], op0=ADD, op1=MULT,
-                    )
-                else:
-                    nc.scalar.activation(
-                        out=y_rows[c][:, t, :], in_=banks[t][:], func=ACT.Identity,
-                        scale=fader_sb[:, t : t + 1], bias=bo_faded[:, t : t + 1],
-                    )
-            nc.sync.dma_start(out=out_0[:, m0 : m0 + w].rearrange("(p t) m -> p t m", t=PACK), in_=y_rows[c][:])
+                nc.scalar.activation(
+                    out=y_rows[c][:, t, :], in_=banks[t][:], func=ACT.Identity,
+                    scale=fader_sb[:, t : t + 1], bias=bo_faded[:, t : t + 1],
+                )
+                if (t + 1) % step == 0:
+                    nc.sync.dma_start(out=out_rows[:, t + 1 - step : t + 1, :], in_=y_rows[c][:, t + 1 - step : t + 1, :])
 
-        saturate(0, slice(0, 2), slice(0, M))
-        z_rows0 = sum_z(0, direct0, 0, M, None, (0, 1))
-        quantise(wd_w[1][:], wd_s[1][:], round_wd(1))
-        direct1 = direct(1)
-        saturate(0, slice(2, 4), slice(0, M))
-        sum_z(0, direct0, 0, M, z_rows0, (2, 3))
-        lo, hi = slice(0, 256), slice(256, 512)
-        saturate(1, slice(0, PACK), lo)
-        z0a = weave(nc.vector.tensor_copy, z_rows0[:, :, lo], "z_woven00")
-        saturate(1, slice(0, PACK), hi)
-        z0b = weave(nc.scalar.copy, z_rows0[:, :, hi], "z_woven01")
+        def weave_y(c):
+            weave_into(nc.vector.tensor_copy, y_woven[:, chunk_cols(c), :], y_rows[c][:])
 
-        rows_a = sum_z(1, direct1, 0, 256)
-        z1a = weave(nc.vector.tensor_copy, rows_a[:], "z_woven10")
-        quantise_z(0, lo, z0a)
-        mix_a = open_mix(0)
-        quantise_z(1, lo, z1a)
-        close_mix(0, mix_a, ())
-        rows_b = sum_z(1, direct1, 256, 256)
-        z1b = weave(nc.vector.tensor_copy, rows_b[:, :, 0:128], "z_woven11")
-        quantise_z(0, hi, z0b)
-        mix_b = open_mix(1)
-        quantise_z(1, chunk_cols(1), z1b)
-        close_mix(1, mix_b, ())
-        z1c = weave(nc.vector.tensor_copy, rows_b[:, :, 128:256], "z_woven12")
-        weave_y(0, nc.vector.tensor_copy)
-        mix_c = open_mix(2)
-        quantise_z(1, chunk_cols(2), z1c)
-        close_mix(2, mix_c, ())
-        store_codes(0, 256)
-        weave_y(1, nc.vector.tensor_copy)
-        weave_y(2, nc.vector.tensor_copy)
-        store_codes(256, 256)
+        def quantise_y(cols):
+            quantise(y_w[:, cols], y_s[:, cols], y_woven[:, cols, :].rearrange("p m t -> p (m t)"))
+
+        def store_codes(cols):
+            nc.sync.dma_start(
+                out=out_1[0].rearrange("p m t -> p (m t)").bitcast(I32)[:, cols], in_=y_w[:, cols].bitcast(I32)
+            )
+
+        saturate(0, 1)
+        saturate(1, 0)
+        saturate(1, 1)
+        rows01 = sum_z(0, 1, direct0)
+        rows10 = sum_z(1, 0, direct1)
+        z01 = weave(nc.scalar.copy, rows01[:], "z_woven01")
+        z10 = weave(nc.vector.tensor_copy, rows10[:], "z_woven10")
+        mix_a = open_mix(0, (4, 5, 0, 1))
+        quantise_z(1, half_cols(0), z10)
+        close_mix(0, mix_a, 2)
+        rows11 = sum_z(1, 1, direct1)
+        z11a = weave(nc.vector.tensor_copy, rows11[:, :, 0:128], "z_woven11a")
+        quantise_z(0, half_cols(1), z01)
+        mix_b = open_mix(1, (6, 7, 2, 3))
+        quantise_z(1, chunk_cols(1), z11a)
+        close_mix(1, mix_b, 1)
+        z11b = weave(nc.vector.tensor_copy, rows11[:, :, 128:256], "z_woven11b")
+        weave_y(0)
+        mix_c = open_mix(2, (4, 5, 0, 1))
+        quantise_z(1, chunk_cols(2), z11b)
+        close_mix(2, mix_c, 1)
+        quantise_y(chunk_cols(0))
+        store_codes(chunk_cols(0))
+        weave_y(1)
+        quantise_y(chunk_cols(1))
+        weave_y(2)
+        quantise_y(chunk_cols(2))
+        store_codes(half_cols(1))
         for q in range(P // QUAD):
             queue = nc.sync if q % 2 == 0 else nc.scalar
             queue.dma_start(

@@ -216,6 +216,18 @@ def tile_list_delay_tap_mixer_kernel(
             if a == 1:
                 nc.scalar.activation(out=h_sb[s][:, BANK * jh : BANK * (jh + 1)], in_=acc[:], func=ACT.Copy)
 
+        idle = bank(7, [P, BANK])
+        for i in range(3):
+            nc.tensor.matmul_mx(
+                out=idle[:],
+                lhsT=w4_w[0][0][:, 0 : 2 * P].bitcast(FP4X4),
+                lhsT_scale=w4_s[0][0][:, 0:P],
+                rhs=v_w[0][0][:].bitcast(FP8X4),
+                rhs_scale=w4_s[0][0][:],
+                start=True,
+                stop=True,
+            )
+
         early = [bank(k, [P, BANK]) for k in range(3)]
         h_pass(early[0], 0, 0, 0)
         h_pass(early[1], 0, 1, 0)

@@ -28,6 +28,7 @@ RUN = 4
 
 
 HALF = M // 2
+LOOKUPS = (((0, 512), (512, 512)), ((0, 256), (256, 256), (512, 512)))
 CHUNKS = ((0, 256), (256, 128), (384, 128))
 
 
@@ -68,7 +69,7 @@ def tile_list_delay_tap_mixer_kernel(
         tab_w = [sbuf([P, T], I32, f"tab_w{a}") for a in range(2)]
         tab_s = sbuf([P, T], U8, "tab_s")
         picked_s = sbuf([P, S], U8, "picked_s")
-        v_w = [[sbuf([P, BANK], U32, f"v_w{a}{jh}") for jh in range(2)] for a in range(2)]
+        v_w = [sbuf([P, S], U32, f"v_w{a}") for a in range(2)]
         v_s = sbuf([P, 2, S], U8, "v_s")
         w4_sraw = sbuf([P, 2, H], U8, "w4_sraw")
         w4_s = [[sbuf([P, PASS], U8, f"w4_s{b}{a}") for a in range(2)] for b in range(2)]
@@ -128,16 +129,17 @@ def tile_list_delay_tap_mixer_kernel(
         for b in range(2):
             for a in range(2):
                 deal_w4_plane(b, a)
-        deal_w4(nc.scalar.copy, 1, 0)
-        deal_w4(nc.gpsimd.tensor_copy, 1, 1)
+        deal_w4(nc.gpsimd.tensor_copy, 1, 0)
 
         for a in range(2):
-            for jh in range(2):
-                entries = list1[:, jh * BANK // GROUP : (jh + 1) * BANK // GROUP]
-                nc.vector.tensor_copy(v_w[a][jh][:], tab_w[a][:].bitcast(U32).indirect(entries))
+            for j0, width in LOOKUPS[a]:
+                entries = list1[:, j0 // GROUP : (j0 + width) // GROUP]
+                nc.vector.tensor_copy(v_w[a][:, j0 : j0 + width], tab_w[a][:].bitcast(U32).indirect(entries))
+
+        deal_w4(nc.vector.tensor_copy, 1, 1)
 
         dry_rows = dry.rearrange("(p j) m -> p j m", j=PACK)
-        dry_lo = sbuf([P, PACK, HALF], F32, "dry_lo", "picked_s")
+        dry_lo = sbuf([P, PACK, HALF], F32, "dry_lo")
         nc.sync.dma_start(out=dry_lo[:], in_=dry_rows[:, :, 0:HALF])
         dry_hi = sbuf([P, PACK, HALF], F32, "dry_hi", "w4_raw0")
         nc.sync.dma_start(out=dry_hi[:], in_=dry_rows[:, :, HALF:M])
@@ -151,7 +153,7 @@ def tile_list_delay_tap_mixer_kernel(
             )
             return rows
 
-        wd_raw = [load_wd(0, "tab_w1"), load_wd(1, "picked_s")]
+        wd_raw = [load_wd(0, "tab_w1"), load_wd(1, "dry_lo")]
 
         vectors = sbuf([P, 3, 2 * PACK], F32, "vectors", "tab_s")
         gain_sb = vectors[:, 0, :]
@@ -202,19 +204,25 @@ def tile_list_delay_tap_mixer_kernel(
 
         h_sb = [sbuf([P, S], F32, f"h_sb{s}") for s in range(6)]
 
-        def h_pass(acc, s, jh, a):
+        def h_pass(acc, s, j0, a):
             b, t = divmod(s, PACK)
+            cols = slice(j0, j0 + acc.shape[1])
             nc.tensor.matmul_mx(
                 out=acc[:],
                 lhsT=w4_w[b][a][:, 2 * P * t : 2 * P * (t + 1)].bitcast(FP4X4),
                 lhsT_scale=w4_s[b][a][:, P * t : P * (t + 1)],
-                rhs=v_w[a][jh][:].bitcast(FP8X4),
-                rhs_scale=v_s[:, a, BANK * jh : BANK * (jh + 1)],
+                rhs=v_w[a][:, cols].bitcast(FP8X4),
+                rhs_scale=v_s[:, a, cols],
                 start=(a == 0),
                 stop=(a == 1),
             )
             if a == 1:
-                nc.scalar.activation(out=h_sb[s][:, BANK * jh : BANK * (jh + 1)], in_=acc[:], func=ACT.Copy)
+                nc.scalar.activation(out=h_sb[s][:, cols], in_=acc[:], func=ACT.Copy)
+
+        def h_sum(k, s, j0, width):
+            acc = bank(k, [P, width])
+            for a in range(2):
+                h_pass(acc, s, j0, a)
 
         idle = bank(7, [P, BANK])
         for i in range(3):
@@ -222,28 +230,21 @@ def tile_list_delay_tap_mixer_kernel(
                 out=idle[:],
                 lhsT=w4_w[0][0][:, 0 : 2 * P].bitcast(FP4X4),
                 lhsT_scale=w4_s[0][0][:, 0:P],
-                rhs=v_w[0][0][:].bitcast(FP8X4),
+                rhs=v_w[0][:, 0:BANK].bitcast(FP8X4),
                 rhs_scale=w4_s[0][0][:],
                 start=True,
                 stop=True,
             )
 
-        early = [bank(k, [P, BANK]) for k in range(3)]
-        h_pass(early[0], 0, 0, 0)
-        h_pass(early[1], 0, 1, 0)
-        h_pass(early[0], 0, 0, 1)
-        h_pass(early[2], 1, 0, 0)
-        h_pass(early[2], 1, 0, 1)
-        h_pass(early[1], 0, 1, 1)
-        for k in range(3, 4 * PACK):
-            s, jh = divmod(k, 2)
-            if k == 12:
+        for k, (s, j0) in enumerate(((0, 0), (1, 0), (0, 256), (1, 256))):
+            h_sum(4 + k, s, j0, 256)
+        wide = [(2, 0), (0, BANK), (1, BANK), (2, BANK)] + [(s, j0) for s in range(3, 2 * PACK) for j0 in (0, BANK)]
+        for k, (s, j0) in enumerate(wide):
+            if (s, j0) == (6, 0):
                 wd_woven0 = round_wd(0)
                 h_sb.append(sbuf([P, S], F32, "h_sb6", "tab_w1"))
                 h_sb.append(sbuf([P, S], F32, "h_sb7"))
-            acc = bank(k % 4, [P, BANK])
-            for a in range(2):
-                h_pass(acc, s, jh, a)
+            h_sum(k % 4, s, j0, BANK)
 
         wm_raw = sbuf([P, 2, N], I32, "wm_raw", "w4_w00")
         nc.sync.dma_start(out=wm_raw[:], in_=wm_words.rearrange("a p c i -> p a (c i)").bitcast(I32))

@@ -141,10 +141,10 @@ def tile_list_delay_tap_mixer_kernel(
         dry_rows = dry.rearrange("(p j) m -> p j m", j=PACK)
         dry_lo = sbuf([P, PACK, HALF], F32, "dry_lo")
         nc.sync.dma_start(out=dry_lo[:], in_=dry_rows[:, :, 0:HALF])
-        dry_hi = sbuf([P, PACK, HALF], F32, "dry_hi", "w4_raw0")
-        nc.sync.dma_start(out=dry_hi[:], in_=dry_rows[:, :, HALF:M])
-        wgt_sb = sbuf([P, M], F32, "wgt_sb", "tab_w0")
+        wgt_sb = sbuf([P, M], F32, "wgt_sb", "w4_raw0")
         nc.sync.dma_start(out=wgt_sb[:], in_=wgt)
+        dry_hi = sbuf([P, PACK, HALF], F32, "dry_hi", "tab_w0")
+        nc.sync.dma_start(out=dry_hi[:], in_=dry_rows[:, :, HALF:M])
 
         def load_wd(b, after):
             rows = sbuf([P, PACK, PASS], F32, f"wd_raw{b}", after)
@@ -167,9 +167,7 @@ def tile_list_delay_tap_mixer_kernel(
 
         dry_w = sbuf([P, M], U32, "dry_w")
         dry_s = sbuf([P, M], U8, "dry_s")
-        dry_woven = sbuf([P, M, PACK], BF16, "dry_woven")
-        weave_into(nc.vector.tensor_copy, dry_woven[:, 0:HALF, :], dry_lo[:])
-        weave_into(nc.vector.tensor_copy, dry_woven[:, HALF:M, :], dry_hi[:])
+        dry_lo_woven = weave(nc.vector.tensor_copy, dry_lo[:], "dry_lo_woven")
 
         wd_w = [sbuf([P, PASS], U32, f"wd_w{b}") for b in range(2)]
         wd_s = [sbuf([P, PASS], U8, f"wd_s{b}") for b in range(2)]
@@ -256,13 +254,16 @@ def tile_list_delay_tap_mixer_kernel(
                 in_=wm_scales[:, QUAD_ROWS * q : QUAD_ROWS * (q + 1), :].bitcast(I32),
             )
 
-        taps = [sbuf([P, PACK, M], F32, "taps0", "w4_raw0"), sbuf([P, PACK, M], F32, "taps1")]
+        taps = [sbuf([P, PACK, M], F32, "taps0"), sbuf([P, PACK, M], F32, "taps1")]
         wet = [sbuf([P, PACK, M], F32, f"wet{b}") for b in range(2)]
         for s in range(2 * PACK):
             b, t = divmod(s, PACK)
             nc.vector.tensor_tensor(taps[b][:, t, :], h_sb[s][:].indirect(list2[:]), wgt_sb[:], MULT)
             if s == 0:
-                quantise(dry_w[:], dry_s[:], dry_woven[:].rearrange("p m t -> p (m t)"))
+                dry_hi_woven = weave(nc.vector.tensor_copy, dry_hi[:], "dry_hi_woven", "h_sb0")
+                quantise(dry_w[:, 0:HALF], dry_s[:, 0:HALF], dry_lo_woven)
+            if s == 1:
+                quantise(dry_w[:, HALF:M], dry_s[:, HALF:M], dry_hi_woven)
             if s == 5:
                 quantise(wd_w[0][:], wd_s[0][:], wd_woven0)
                 direct0 = direct(0, 4)

@@ -98,7 +98,7 @@ def tile_list_delay_tap_mixer_kernel(
         load_table(0)
         w4_raw = [load_w4(0)]
         for r in range(QUAD_ROWS):
-            nc.sync.dma_start(
+            nc.scalar.dma_start(
                 out=w4_sraw[r:P:QUAD, :, :].bitcast(I32),
                 in_=w4_scales.rearrange("a (q r) c -> r q a c", r=QUAD_ROWS)[r].bitcast(I32),
             )
@@ -292,15 +292,14 @@ def tile_list_delay_tap_mixer_kernel(
         def quantise_z(b, cols, woven):
             quantise(z_w[b][:, cols], z_s[b][:, cols], woven)
 
+        wm_cols = wm_raw[:].rearrange("p a (m t) -> p a t m", t=PACK)
+        wm_first = sbuf([P, 2, P], I32, "wm_first", "tab_w1")
         saturate(0, 0)
-        z00 = weave(nc.vector.tensor_copy, sum_z(0, 0, direct0)[:], "z_woven00")
+        rows00 = sum_z(0, 0, direct0)
+        nc.vector.tensor_copy(out=wm_first[:], in_=wm_cols[:, 0, 0:2, :])
         quantise(wd_w[1][:], wd_s[1][:], round_wd(1))
         direct1 = direct(1, 0)
-        wm_cols = wm_raw[:].rearrange("p a (m t) -> p a t m", t=PACK)
-        wm_first = sbuf([P, 2, P], I32, "wm_first", "wd_woven1")
-        nc.vector.tensor_copy(out=wm_first[:], in_=wm_cols[:, 0, 0:2, :])
-        quantise_z(0, half_cols(0), z00)
-        wm_rest = sbuf([P, 6, P], I32, "wm_rest", "z_woven00")
+        wm_rest = sbuf([P, 6, P], I32, "wm_rest", "wd_woven1")
         nc.gpsimd.tensor_copy(out=wm_rest[:, 0:2, :], in_=wm_cols[:, 0, 2:4, :])
         nc.gpsimd.tensor_copy(out=wm_rest[:, 2:6, :], in_=wm_cols[:, 1, :, :])
         wm_w = [wm_first[:, 0, :], wm_first[:, 1, :]] + [wm_rest[:, i, :] for i in range(6)]
@@ -355,11 +354,13 @@ def tile_list_delay_tap_mixer_kernel(
 
         saturate(0, 1)
         saturate(1, 0)
+        z00 = weave(nc.scalar.copy, rows00[:], "z_woven00")
         saturate(1, 1)
         rows01 = sum_z(0, 1, direct0)
         rows10 = sum_z(1, 0, direct1)
         z01 = weave(nc.scalar.copy, rows01[:], "z_woven01")
         z10 = weave(nc.vector.tensor_copy, rows10[:], "z_woven10")
+        quantise_z(0, half_cols(0), z00)
         mix_a = open_mix(0, (4, 5, 0, 1))
         quantise_z(1, half_cols(0), z10)
         close_mix(0, mix_a, 2)

from contextlib import ExitStack

import concourse.mybir as mybir

K, K2, H, N, T, S, M = 1024, 512, 1024, 512, 2048, 1024, 512
FLOPS = 2 * (K * H * S + K2 * H * M + H * N * M)

F32 = mybir.dt.float32
BF16 = mybir.dt.bfloat16
I32 = mybir.dt.int32
U32 = mybir.dt.uint32
U16 = mybir.dt.uint16
U8 = mybir.dt.uint8
FP8X4 = mybir.dt.float8_e4m3fn_x4
FP4X4 = mybir.dt.float4_e2m1fn_x4
MULT = mybir.AluOpType.mult
ADD = mybir.AluOpType.add
ACT = mybir.ActivationFunctionType

P = 128
PACK = 4
PASS = P * PACK
BANK = 512
GROUP = 16
QUAD = 32
QUAD_ROWS = 4
RUN = 4


HALF = M // 2
LOOKUPS = (((0, 512), (512, 512)), ((0, 256), (256, 256), (512, 512)))
CHUNKS = ((0, 256), (256, 128), (384, 128))


def tile_list_delay_tap_mixer_kernel(
    tc, tab_words, tab_scales, offs, w4_words, w4_scales, offs2, wgt, gain, dry, wd,
    wm_words, wm_scales, bo, fader, out_0, out_1, out_2,
):
    nc = tc.nc
    with ExitStack() as ctx:
        held = ctx.enter_context(tc.tile_pool(name="held", bufs=1))
        psum = ctx.enter_context(tc.psum_pool(name="psum", bufs=1))

        def sbuf(shape, dtype, name, after=None):
            return held.tile(shape, dtype, name=name, tag=after or name, align_bytes=64)

        def bank(k, shape):
            return psum.tile(shape, F32, name=f"bank{k}", tag=f"bank{k}")

        def quantise(words, plane, woven):
            nc.vector.quantize_mx(out=words.bitcast(FP8X4), scales=plane, in_=woven)

        def weave_into(copy, woven, rows):
            copy(
                out=woven.rearrange("p (c i) t -> p c t i", i=RUN),
                in_=rows.rearrange("p t (c i) -> p c t i", i=RUN),
            )

        def weave(copy, rows, name, after=None):
            woven = sbuf([P, rows.shape[2], PACK], BF16, name, after)
            weave_into(copy, woven[:], rows)
            return woven[:].rearrange("p m t -> p (m t)")

        def deal(copy, dealt, raw):
            copy(out=dealt, in_=raw.rearrange("p (m t) -> p t m", t=PACK))

        list1 = held.tile([P, S // GROUP], U16, name="list1")
        list2 = held.tile([P, M // GROUP], U16, name="list2")
        tab_w = [sbuf([P, T], I32, f"tab_w{a}") for a in range(2)]
        tab_s = sbuf([P, T], U8, "tab_s")
        picked_s = sbuf([P, S], U8, "picked_s")
        v_w = [sbuf([P, S], U32, f"v_w{a}") for a in range(2)]
        v_s = sbuf([P, 2, S], U8, "v_s")
        w4_sraw = sbuf([P, 2, H], U8, "w4_sraw")
        w4_s = [[sbuf([P, PASS], U8, f"w4_s{b}{a}") for a in range(2)] for b in range(2)]
        w4_w = [[sbuf([P, 2 * PASS], U8, f"w4_w{b}{a}") for a in range(2)] for b in range(2)]
        rows0 = P - QUAD

        nc.gpsimd.memset(w4_sraw[:].bitcast(I32), 0)
        nc.vector.memset(tab_s[0:rows0, :].bitcast(I32), 0)
        nc.gpsimd.memset(v_s[:].bitcast(I32), 0)

        def load_w4(b, after=None):
            raw = sbuf([P, 2, 2 * PASS], U8, f"w4_raw{b}", after)
            nc.sync.dma_start(
                out=raw[:].bitcast(I32),
                in_=w4_words[:, :, 2 * PASS * b : 2 * PASS * (b + 1)].rearrange("a p c -> p a c").bitcast(I32),
            )
            return raw

        def load_table(a):
            nc.sync.dma_start(out=tab_w[a][:], in_=tab_words[a].rearrange("p t i -> p (t i)").bitcast(I32))

        nc.sync.dma_start(list1[:], offs)
        nc.sync.dma_start(
            out=tab_s[rows0:P, :].bitcast(I32), in_=tab_scales.rearrange("a q c -> q a c").bitcast(I32)
        )
        load_table(0)
        w4_raw = [load_w4(0)]
        for r in range(QUAD_ROWS):
            nc.scalar.dma_start(
                out=w4_sraw[r:P:QUAD, :, :].bitcast(I32),
                in_=w4_scales.rearrange("a (q r) c -> r q a c", r=QUAD_ROWS)[r].bitcast(I32),
            )
        load_table(1)
        nc.sync.dma_start(list2[:], offs2)

        nc.vector.tensor_copy(picked_s[:], tab_s[:].indirect(list1[:]))
        for q in range(P // QUAD):
            first = rows0 + 2 * QUAD_ROWS * q
            nc.sync.dma_start(
                out=v_s[QUAD * q : QUAD * q + QUAD_ROWS, :, :].bitcast(I32),
                in_=picked_s[first : first + 2 * QUAD_ROWS, :].bitcast(I32),
            )
        w4_raw.append(load_w4(1, "tab_s"))

        def deal_w4(copy, b, a):
            deal(copy, w4_w[b][a][:].bitcast(U16).rearrange("p (t m) -> p t m", t=PACK), w4_raw[b][:, a, :].bitcast(U16))

        def deal_w4_plane(b, a):
            deal(
                nc.gpsimd.tensor_copy,
                w4_s[b][a][:].rearrange("p (t m) -> p t m", t=PACK),
                w4_sraw[:, a, PASS * b : PASS * (b + 1)],
            )

        for a in range(2):
            deal_w4(nc.scalar.copy, 0, a)
        for b in range(2):
            for a in range(2):
                deal_w4_plane(b, a)
        deal_w4(nc.gpsimd.tensor_copy, 1, 0)

        for a in range(2):
            for j0, width in LOOKUPS[a]:
                entries = list1[:, j0 // GROUP : (j0 + width) // GROUP]
                nc.vector.tensor_copy(v_w[a][:, j0 : j0 + width], tab_w[a][:].bitcast(U32).indirect(entries))

        deal_w4(nc.vector.tensor_copy, 1, 1)

        dry_rows = dry.rearrange("(p j) m -> p j m", j=PACK)
        dry_lo = sbuf([P, PACK, HALF], F32, "dry_lo")
        nc.sync.dma_start(out=dry_lo[:], in_=dry_rows[:, :, 0:HALF])
        wgt_sb = sbuf([P, M], F32, "wgt_sb", "w4_raw0")
        nc.sync.dma_start(out=wgt_sb[:], in_=wgt)
        dry_hi = sbuf([P, PACK, HALF], F32, "dry_hi", "tab_w0")
        nc.sync.dma_start(out=dry_hi[:], in_=dry_rows[:, :, HALF:M])

        def load_wd(b, after):
            rows = sbuf([P, PACK, PASS], F32, f"wd_raw{b}", after)
            nc.sync.dma_start(
                out=rows[:], in_=wd[:, PASS * b : PASS * (b + 1)].rearrange("(p j) c -> p j c", j=PACK)
            )
            return rows

        wd_raw = [load_wd(0, "tab_w1"), load_wd(1, "dry_lo")]

        vectors = sbuf([P, 3, 2 * PACK], F32, "vectors", "tab_s")
        gain_sb = vectors[:, 0, :]
        bo_sb = vectors[:, 1, 0:PACK]
        fader_sb = vectors[:, 2, 0:PACK]
        nc.sync.dma_start(
            out=gain_sb.rearrange("p (b t) -> p b t", t=PACK), in_=gain.rearrange("(b p t) -> p b t", b=2, t=PACK)
        )
        nc.sync.dma_start(out=bo_sb, in_=bo.rearrange("(p t) -> p t", t=PACK))
        nc.sync.dma_start(out=fader_sb, in_=fader.rearrange("(p t) -> p t", t=PACK))

        dry_w = sbuf([P, M], U32, "dry_w")
        dry_s = sbuf([P, M], U8, "dry_s")
        dry_lo_woven = weave(nc.vector.tensor_copy, dry_lo[:], "dry_lo_woven")

        wd_w = [sbuf([P, PASS], U32, f"wd_w{b}") for b in range(2)]
        wd_s = [sbuf([P, PASS], U8, f"wd_s{b}") for b in range(2)]

        def round_wd(b):
            woven = sbuf([P, PACK, P, PACK], BF16, f"wd_woven{b}")
            nc.scalar.copy(
                out=woven[:].rearrange("p t m j -> p m j t"),
                in_=wd_raw[b][:].rearrange("p j (m t) -> p m j t", t=PACK),
            )
            return woven[:].rearrange("p t m j -> p (t m j)")

        def half_cols(x):
            return slice(HALF * x, HALF * (x + 1))

        def direct(b, first_bank):
            sums = []
            for x in range(2):
                pairs = [bank(first_bank + 2 * x + u, [P, 2, HALF]) for u in range(2)]
                for t in range(PACK):
                    nc.tensor.matmul_mx(
                        out=pairs[t // 2][:, t % 2, :],
                        lhsT=wd_w[b][:, P * t : P * (t + 1)].bitcast(FP8X4),
                        lhsT_scale=wd_s[b][:, P * t : P * (t + 1)],
                        rhs=dry_w[:, half_cols(x)].bitcast(FP8X4),
                        rhs_scale=dry_s[:, half_cols(x)],
                        start=True,
                        stop=True,
                    )
                sums.append([pairs[t // 2][:, t % 2, :] for t in range(PACK)])
            return sums

        h_sb = [sbuf([P, S], F32, f"h_sb{s}") for s in range(6)]

        def h_pass(acc, s, j0, a):
            b, t = divmod(s, PACK)
            cols = slice(j0, j0 + acc.shape[1])
            nc.tensor.matmul_mx(
                out=acc[:],
                lhsT=w4_w[b][a][:, 2 * P * t : 2 * P * (t + 1)].bitcast(FP4X4),
                lhsT_scale=w4_s[b][a][:, P * t : P * (t + 1)],
                rhs=v_w[a][:, cols].bitcast(FP8X4),
                rhs_scale=v_s[:, a, cols],
                start=(a == 0),
                stop=(a == 1),
            )
            if a == 1:
                nc.scalar.activation(out=h_sb[s][:, cols], in_=acc[:], func=ACT.Copy)

        def h_sum(k, s, j0, width):
            acc = bank(k, [P, width])
            for a in range(2):
                h_pass(acc, s, j0, a)

        idle = bank(7, [P, BANK])
        for i in range(3):
            nc.tensor.matmul_mx(
                out=idle[:],
                lhsT=w4_w[0][0][:, 0 : 2 * P].bitcast(FP4X4),
                lhsT_scale=w4_s[0][0][:, 0:P],
                rhs=v_w[0][:, 0:BANK].bitcast(FP8X4),
                rhs_scale=w4_s[0][0][:],
                start=True,
                stop=True,
            )

        for k, (s, j0) in enumerate(((0, 0), (1, 0), (0, 256), (1, 256))):
            h_sum(4 + k, s, j0, 256)
        wide = [(2, 0), (0, BANK), (1, BANK), (2, BANK)] + [(s, j0) for s in range(3, 2 * PACK) for j0 in (0, BANK)]
        for k, (s, j0) in enumerate(wide):
            if (s, j0) == (6, 0):
                wd_woven0 = round_wd(0)
                h_sb.append(sbuf([P, S], F32, "h_sb6", "tab_w1"))
                h_sb.append(sbuf([P, S], F32, "h_sb7"))
            h_sum(k % 4, s, j0, BANK)

        wm_raw = sbuf([P, 2, N], I32, "wm_raw", "w4_w00")
        nc.sync.dma_start(out=wm_raw[:], in_=wm_words.rearrange("a p c i -> p a (c i)").bitcast(I32))
        wm_sraw = sbuf([P, N], U8, "wm_sraw", "w4_sraw")
        nc.gpsimd.memset(wm_sraw[:].bitcast(I32), 0)
        for q in range(P // QUAD):
            nc.sync.dma_start(
                out=wm_sraw[QUAD * q : QUAD * q + 2 * QUAD_ROWS, :].bitcast(I32),
                in_=wm_scales[:, QUAD_ROWS * q : QUAD_ROWS * (q + 1), :].bitcast(I32),
            )

        taps = [sbuf([P, PACK, M], F32, "taps0"), sbuf([P, PACK, M], F32, "taps1")]
        wet = [sbuf([P, PACK, M], F32, f"wet{b}") for b in range(2)]
        for s in range(2 * PACK):
            b, t = divmod(s, PACK)
            nc.vector.tensor_tensor(taps[b][:, t, :], h_sb[s][:].indirect(list2[:]), wgt_sb[:], MULT)
            if s == 0:
                dry_hi_woven = weave(nc.vector.tensor_copy, dry_hi[:], "dry_hi_woven", "h_sb0")
                quantise(dry_w[:, 0:HALF], dry_s[:, 0:HALF], dry_lo_woven)
            if s == 1:
                quantise(dry_w[:, HALF:M], dry_s[:, HALF:M], dry_hi_woven)
            if s == 5:
                quantise(wd_w[0][:], wd_s[0][:], wd_woven0)
                direct0 = direct(0, 4)
        bo_faded = sbuf([P, PACK], F32, "bo_faded", "h_sb4")
        nc.vector.tensor_tensor(bo_faded[:], bo_sb, fader_sb, MULT)

        wm_s = sbuf([P, N], U8, "wm_s", "h_sb7")
        deal(nc.gpsimd.tensor_copy, wm_s[:].rearrange("p (t m) -> p t m", t=PACK), wm_sraw[:])

        def saturate(b, x):
            nc.scalar.activation(out=wet[b][:, :, half_cols(x)], in_=taps[b][:, :, half_cols(x)], func=ACT.Tanh)

        def sum_z(b, x, sums):
            z_rows = sbuf([P, PACK, HALF], BF16, f"z_rows{b}{x}")
            for t in range(PACK):
                s = PACK * b + t
                nc.vector.scalar_tensor_tensor(
                    out=z_rows[:, t, :], in0=wet[b][:, t, half_cols(x)], scalar=gain_sb[:, s : s + 1], in1=sums[x][t],
                    op0=MULT, op1=ADD,
                )
            return z_rows

        z_w = [sbuf([P, M], U32, f"z_w{b}") for b in range(2)]
        z_s = [sbuf([P, M], U8, f"z_s{b}") for b in range(2)]

        def quantise_z(b, cols, woven):
            quantise(z_w[b][:, cols], z_s[b][:, cols], woven)

        wm_cols = wm_raw[:].rearrange("p a (m t) -> p a t m", t=PACK)
        wm_first = sbuf([P, 2, P], I32, "wm_first", "tab_w1")
        saturate(0, 0)
        rows00 = sum_z(0, 0, direct0)
        nc.vector.tensor_copy(out=wm_first[:], in_=wm_cols[:, 0, 0:2, :])
        quantise(wd_w[1][:], wd_s[1][:], round_wd(1))
        direct1 = direct(1, 0)
        wm_rest = sbuf([P, 6, P], I32, "wm_rest", "wd_woven1")
        nc.gpsimd.tensor_copy(out=wm_rest[:, 0:2, :], in_=wm_cols[:, 0, 2:4, :])
        nc.gpsimd.tensor_copy(out=wm_rest[:, 2:6, :], in_=wm_cols[:, 1, :, :])
        wm_w = [wm_first[:, 0, :], wm_first[:, 1, :]] + [wm_rest[:, i, :] for i in range(6)]

        y_rows = [sbuf([P, PACK, w], F32, f"y_rows{c}") for c, (m0, w) in enumerate(CHUNKS)]
        y_woven = sbuf([P, M, PACK], BF16, "y_woven")
        y_w = sbuf([P, M], U32, "y_w")
        y_s = sbuf([P, M], U8, "y_s")

        def chunk_cols(c):
            return slice(CHUNKS[c][0], CHUNKS[c][0] + CHUNKS[c][1])

        def mix_pass(acc, c, t, b):
            nc.tensor.matmul_mx(
                out=acc[:],
                lhsT=wm_w[PACK * b + t].bitcast(FP8X4),
                lhsT_scale=wm_s[QUAD_ROWS * b : P, P * t : P * (t + 1)],
                rhs=z_w[b][:, chunk_cols(c)].bitcast(FP8X4),
                rhs_scale=z_s[b][:, chunk_cols(c)],
                start=(b == 0),
                stop=(b == 1),
            )

        def open_mix(c, free):
            banks = [bank(k, [P, CHUNKS[c][1]]) for k in free]
            for t in range(PACK):
                mix_pass(banks[t], c, t, 0)
            return banks

        def close_mix(c, banks, parts):
            out_rows = out_0[:, chunk_cols(c)].rearrange("(p t) m -> p t m", t=PACK)
            step = PACK // parts
            for t in range(PACK):
                mix_pass(banks[t], c, t, 1)
                nc.scalar.activation(
                    out=y_rows[c][:, t, :], in_=banks[t][:], func=ACT.Identity,
                    scale=fader_sb[:, t : t + 1], bias=bo_faded[:, t : t + 1],
                )
                if (t + 1) % step == 0:
                    nc.sync.dma_start(out=out_rows[:, t + 1 - step : t + 1, :], in_=y_rows[c][:, t + 1 - step : t + 1, :])

        def weave_y(c):
            weave_into(nc.vector.tensor_copy, y_woven[:, chunk_cols(c), :], y_rows[c][:])

        def quantise_y(cols):
            quantise(y_w[:, cols], y_s[:, cols], y_woven[:, cols, :].rearrange("p m t -> p (m t)"))

        def store_codes(cols):
            nc.sync.dma_start(
                out=out_1[0].rearrange("p m t -> p (m t)").bitcast(I32)[:, cols], in_=y_w[:, cols].bitcast(I32)
            )

        saturate(0, 1)
        saturate(1, 0)
        z00 = weave(nc.scalar.copy, rows00[:], "z_woven00")
        saturate(1, 1)
        rows01 = sum_z(0, 1, direct0)
        rows10 = sum_z(1, 0, direct1)
        z01 = weave(nc.scalar.copy, rows01[:], "z_woven01")
        z10 = weave(nc.vector.tensor_copy, rows10[:], "z_woven10")
        quantise_z(0, half_cols(0), z00)
        mix_a = open_mix(0, (4, 5, 0, 1))
        quantise_z(1, half_cols(0), z10)
        close_mix(0, mix_a, 2)
        rows11 = sum_z(1, 1, direct1)
        z11a = weave(nc.vector.tensor_copy, rows11[:, :, 0:128], "z_woven11a")
        quantise_z(0, half_cols(1), z01)
        mix_b = open_mix(1, (6, 7, 2, 3))
        quantise_z(1, chunk_cols(1), z11a)
        close_mix(1, mix_b, 1)
        z11b = weave(nc.vector.tensor_copy, rows11[:, :, 128:256], "z_woven11b")
        weave_y(0)
        mix_c = open_mix(2, (4, 5, 0, 1))
        quantise_z(1, chunk_cols(2), z11b)
        close_mix(2, mix_c, 1)
        quantise_y(chunk_cols(0))
        store_codes(chunk_cols(0))
        weave_y(1)
        quantise_y(chunk_cols(1))
        weave_y(2)
        quantise_y(chunk_cols(2))
        store_codes(half_cols(1))
        for q in range(P // QUAD):
            queue = nc.sync if q % 2 == 0 else nc.scalar
            queue.dma_start(
                out=out_2[0, QUAD_ROWS * q : QUAD_ROWS * (q + 1), :].bitcast(I32),
                in_=y_s[QUAD * q : QUAD * q + QUAD_ROWS, :].bitcast(I32),
            )
